import numpy as np
import ml_dtypes


def mxq(x, axis, fmt="e4m3"):
    dtype, down = {"e4m3": (ml_dtypes.float8_e4m3fn, 7), "e5m2": (ml_dtypes.float8_e5m2, 14)}[fmt]
    v = np.moveaxis(np.asarray(x, np.float32).astype(ml_dtypes.bfloat16).astype(np.float64), axis, -1)
    blocks = v.reshape(v.shape[:-1] + (-1, 32))
    amax = np.abs(blocks).max(-1, keepdims=True)
    byte = np.maximum(np.where(amax > 0, np.frexp(amax)[1] - 1 + 127, 0) - down, 1)
    scale = np.exp2(byte - 127.0)
    codes = (blocks / scale).astype(np.float32).astype(dtype).astype(np.float64)
    return np.moveaxis((codes * scale).reshape(v.shape), -1, axis)


WIDE = False


def mx_kscale(k):
    if not WIDE:
        return np.ones(k)
    levels = np.array([10, -10, 5, -5, 0])
    if k % 512:
        return np.exp2(np.random.permutation(np.resize(levels, k // 32))).repeat(32)
    a = np.empty((k // 512, 16))
    for p in range(k // 512):
        a[p, :8] = np.random.permutation(np.resize(levels, 8))
        for g in range(8):
            far = levels[np.abs(levels - a[p, g]) >= 10]
            a[p, g + 8] = far[np.random.randint(len(far))]
    return np.exp2(a.ravel()).repeat(32)


def f64(x):
    return np.asarray(x).astype(np.float64)


def striped(idx):
    return np.tile(idx.reshape(-1, 16).T, (8, 1)).astype(np.uint16)


def unstriped(offs):
    return offs[:16].T.reshape(-1).astype(np.int64)


E2M1 = np.array([0.0, 0.5, 1.0, 1.5, 2.0, 3.0, 4.0, 6.0, -0.0, -0.5, -1.0, -1.5, -2.0, -3.0, -4.0, -6.0])


def pack_weight(w, fmt):
    k, n = w.shape
    w = f64(np.asarray(w, np.float32).astype(ml_dtypes.bfloat16)).reshape(k // 32, 32, n)
    amax = np.abs(w).max(1)
    if fmt == "e4m3":
        byte = np.frexp(amax)[1] - 1 + 127 - 7
    else:
        mant, ex = np.frexp(amax / 6.0)
        byte = np.where(mant > 0.5, ex, ex - 1) + 127
    byte = np.clip(np.where(amax > 0, byte, 1), 1, 254)
    scaled = (w * np.exp2(127.0 - byte)[:, None, :]).reshape(k, n).astype(np.float32)
    by_word = np.ascontiguousarray(scaled.reshape(k // 512, 128, 4, n).transpose(0, 1, 3, 2))
    if fmt == "e4m3":
        words = by_word.astype(ml_dtypes.float8_e4m3fn).view(np.uint8)
    else:
        c = by_word.astype(ml_dtypes.float4_e2m1fn).view(np.uint8) & 0xF
        words = (c[..., 0::2] | (c[..., 1::2] << 4)).reshape(k // 512, 128, 2 * n)
    return np.ascontiguousarray(words), np.ascontiguousarray(byte.astype(np.uint8).reshape(k // 512, 16, n))


def unpack_weight(words, scales, fmt):
    g, _, n = scales.shape
    words = np.ascontiguousarray(words).reshape(g, 128, n, -1)
    if fmt == "e4m3":
        vals = words.view(ml_dtypes.float8_e4m3fn).astype(np.float64)
    else:
        nib = np.empty((g, 128, n, 4), np.uint8)
        nib[..., 0::2] = words & 0xF
        nib[..., 1::2] = words >> 4
        vals = E2M1[nib]
    vals = vals * np.repeat(np.exp2(scales.astype(np.float64) - 127.0), 8, axis=1)[..., None]
    return vals.transpose(0, 1, 3, 2).reshape(g * 512, n)


def gelu(v):
    return 0.5 * v * (1.0 + np.tanh(np.sqrt(2.0 / np.pi) * (v + 0.044715 * v**3)))


def bf(x):
    return np.asarray(x, np.float32).astype(ml_dtypes.bfloat16)

def planes(Y):
    n, m = Y.shape
    b = f64(bf(Y)).reshape(n // 32, 32, m)
    amax = np.abs(b).max(1)
    byte = np.clip(np.where(amax > 0, np.frexp(amax)[1] - 1 + 127 - 7, 1), 1, 254)
    codes = (b * np.exp2(127.0 - byte)[:, None, :]).reshape(n, m).astype(np.float32).astype(ml_dtypes.float8_e4m3fn).view(np.uint8)
    words = codes.reshape(n // 512, 128, 4, m).transpose(0, 1, 3, 2)
    return np.ascontiguousarray(words), np.ascontiguousarray(byte.astype(np.uint8).reshape(n // 512, 16, m))


K, T, S, H, N = 512, 4096, 1024, 1024, 512

def setup_inputs():
    n = np.random.standard_normal
    s = mx_kscale(K)[:, None]
    u = mx_kscale(H)[:, None]
    size = np.exp(0.8 * n(N))
    tab_words, tab_scales = pack_weight(n((K, T)) * s, "e4m3")
    w1 = n((K, H)) / np.sqrt(K) / s
    w2_words, w2_scales = pack_weight(n((K, H)) / np.sqrt(K) / s, "e2m1")
    w3_words, w3_scales = pack_weight(n((K, H)) / np.sqrt(K) / s * u.T, "e4m3")
    w4 = n((H, N)) / np.sqrt(H) / u * size[None, :]
    gain = np.exp(0.3 * n(H)) * u[:, 0]
    bias = 0.3 * n(N) * size
    perm = np.random.permutation(T)
    return {"tab_words": tab_words, "tab_scales": tab_scales,
            "offs": striped(perm[:S]), "offs2": striped(perm[S:2 * S]), "offs3": striped(perm[2 * S:3 * S]),
            "w1": w1.astype(np.float32), "w2_words": w2_words, "w2_scales": w2_scales,
            "w3_words": w3_words, "w3_scales": w3_scales, "w4": w4.astype(np.float32),
            "gain": gain.astype(np.float32), "bias": bias.astype(np.float32)}

def reference(tab_words, tab_scales, offs, offs2, offs3, w1, w2_words, w2_scales, w3_words, w3_scales, w4, gain, bias):
    vr = unpack_weight(tab_words, tab_scales, "e4m3")[:, unstriped(offs)]
    vq = unpack_weight(tab_words, tab_scales, "e4m3")[:, unstriped(offs2)]
    va = unpack_weight(tab_words, tab_scales, "e4m3")[:, unstriped(offs3)]
    w2 = unpack_weight(w2_words, w2_scales, "e2m1")
    w3 = unpack_weight(w3_words, w3_scales, "e4m3")
    a = mxq(f64(w1), 0, "e4m3").T @ vr
    b = w2.T @ vq
    c = w3.T @ va
    h = f64(gain)[:, None] * np.tanh(a * b) + c
    y = (mxq(f64(w4), 0, "e4m3").T @ mxq(h, 0, "e4m3")) + f64(bias)[:, None]
    words, scales = planes(y)
    return y, words, scales

@@ -1,0 +1,374 @@
+from contextlib import ExitStack
+
+import concourse.mybir as mybir
+
+K, T, S, H, N = 512, 4096, 1024, 1024, 512
+FLOPS = 2 * (3 * K * H * S + H * N * S)
+
+F32 = mybir.dt.float32
+BF16 = mybir.dt.bfloat16
+I32 = mybir.dt.int32
+U32 = mybir.dt.uint32
+U16 = mybir.dt.uint16
+U8 = mybir.dt.uint8
+FP8X4 = mybir.dt.float8_e4m3fn_x4
+FP4X4 = mybir.dt.float4_e2m1fn_x4
+ACT = mybir.ActivationFunctionType
+ALU = mybir.AluOpType
+
+P = 128
+PASS = 512
+HALF = 512
+W = 256
+UNITS = [(0, 0), (0, 1), (1, 0), (1, 1), (0, 2), (1, 2), (0, 3), (1, 3)]
+GAIN_ENG = ["gggg"] * 8
+YCAST_ENG = "vsvv"
+W4_PIN = {}
+A_PIN = {0: "w3_s", 2: "got_w01", 4: "got_w11", 6: "got_w21"}
+W1_PIN = {(0, 0): "got_w00", (0, 1): "got_w10"}
+TH_FROM = 3
+AB_FROM = 5
+W4_ENG = "s"
+
+
+def tile_list_region_question_answer_kernel(
+    tc, tab_words, tab_scales, offs, offs2, offs3, w1, w2_words, w2_scales, w3_words, w3_scales, w4, gain, bias,
+    out_0, out_1, out_2,
+):
+    nc = tc.nc
+    with ExitStack() as ctx:
+        keep = ctx.enter_context(tc.tile_pool(name="keep", bufs=1))
+        ring = ctx.enter_context(tc.tile_pool(name="ring", bufs=3))
+        psum = ctx.enter_context(tc.psum_pool(name="psum", bufs=2))
+
+        def load_scales(queue, plane, rows):
+            for q in range(4):
+                queue.dma_start(out=plane[32 * q : 32 * q + 4, :].bitcast(I32), in_=rows[0, 4 * q : 4 * q + 4, :].bitcast(I32))
+
+        lists = []
+        for i, src in enumerate((offs, offs2, offs3)):
+            lst = keep.tile([P, S // 16], U16, name=f"list{i}")
+            nc.sync.dma_start(lst[:], src)
+            lists.append(lst)
+        tab_s = keep.tile([P, T], U8, name="tab_s", align_bytes=64)
+        nc.vector.memset(tab_s[:].bitcast(I32), 0)
+        load_scales(nc.sync, tab_s, tab_scales)
+        ident = keep.tile([P, P], F32, name="ident")
+        with tc.tile_pool(name="setup", bufs=1) as setup:
+            zeros = setup.tile([P, P], F32, name="zeros")
+            nc.vector.memset(zeros[:], 0.0)
+            nc.gpsimd.affine_select(
+                out=ident[:], in_=zeros[:], compare_op=ALU.not_equal, fill=1.0, base=0, pattern=[[-1, P]], channel_multiplier=1
+            )
+        stage = ctx.enter_context(tc.tile_pool(name="stage", bufs=1))
+        reuse = ctx.enter_context(tc.tile_pool(name="reuse", bufs=1))
+
+        w1_raw = [stage.tile([P, 4, PASS], F32, name=f"w1_raw{b}") for b in range(2)]
+        w1_rows = w1.rearrange("(p j) c -> p j c", j=4)
+        nc.sync.dma_start(out=w1_raw[0][:], in_=w1_rows[:, :, 0:PASS])
+        tab_w = stage.tile([P, T], U32, name="tab_w", align_bytes=64)
+        nc.sync.dma_start(out=tab_w[:].bitcast(I32), in_=tab_words[0].rearrange("p n t -> p (n t)").bitcast(I32))
+        w2_raw = stage.tile([P, H // 2], I32, name="w2_raw")
+        nc.sync.dma_start(out=w2_raw[:], in_=w2_words[0].bitcast(I32))
+        gain_rows = stage.tile([P, 2 * P], F32, name="gain_rows")
+        nc.vector.memset(gain_rows[:], 0.0)
+        nc.sync.dma_start(
+            out=gain_rows[0:4, :].rearrange("t (g e) -> t g e", e=4),
+            in_=gain.rearrange("(g t e) -> t g e", t=4, e=4),
+        )
+        w2_sraw = stage.tile([P, H], U8, name="w2_sraw")
+        nc.vector.memset(w2_sraw[:].bitcast(I32), 0)
+        load_scales(nc.sync, w2_sraw, w2_scales)
+        w3_raw = stage.tile([P, H], I32, name="w3_raw")
+        nc.sync.dma_start(out=w3_raw[:], in_=w3_words[0].rearrange("p n t -> p (n t)").bitcast(I32))
+        w3_sraw = stage.tile([P, H], U8, name="w3_sraw")
+        nc.vector.memset(w3_sraw[:].bitcast(I32), 0)
+        load_scales(nc.sync, w3_sraw, w3_scales)
+        nc.sync.dma_start(out=w1_raw[1][:], in_=w1_rows[:, :, PASS : 2 * PASS])
+        w4_raw = [reuse.tile([P, 4, N], F32, name=f"w4_raw{b}", offset=8192 * b) for b in range(2)]
+        for b in range(2):
+            rows = w4[PASS * b : PASS * (b + 1), :].rearrange("(q t e) n -> e q t n", t=4, e=4)
+            for e in range(4):
+                nc.sync.dma_start(out=w4_raw[b][e:P:4, :, :], in_=rows[e])
+        bias_col = stage.tile([P, 4], F32, name="bias_col")
+        nc.sync.dma_start(out=bias_col[:], in_=bias.rearrange("(p s) -> p s", s=4))
+
+
+        warm_in = keep.tile([P, 1], F32, name="warm_in")
+        warm_out = keep.tile([P, 1], F32, name="warm_out")
+        nc.vector.memset(warm_in[:], 0.0)
+        nc.scalar.activation(out=warm_out[:], in_=warm_in[:], func=ACT.Tanh)
+
+        got_s = []
+        for i in range(3):
+            g = keep.tile([P, S], U8, name=f"got_s{i}", align_bytes=64)
+            nc.vector.tensor_copy(g[:], tab_s[:].indirect(lists[i][:]))
+            got_s.append(g)
+
+        w1_q = [[None] * 2, [None] * 2]
+
+        def prepare_w1(b):
+            for u in range(2):
+                grouped = keep.tile([P, 1024], BF16, name=f"w1_grouped{b}{u}", tag=W1_PIN.get((b, u), f"w1_grouped{b}{u}"), align_bytes=64)
+                for tt in range(2):
+                    t = 2 * u + tt
+                    nc.scalar.copy(
+                        out=grouped[:, PASS * tt : PASS * (tt + 1)].rearrange("p (q e j) -> p q j e", e=4, j=4),
+                        in_=w1_raw[b][:].rearrange("p j (q t e) -> p t q j e", t=4, e=4)[:, t],
+                    )
+                codes = keep.tile([P, 2 * P], U32, name=f"w1_codes{b}{u}", align_bytes=64)
+                scales = keep.tile([P, 2 * P], U8, name=f"w1_scales{b}{u}", align_bytes=64)
+                nc.vector.quantize_mx(out=codes[:].bitcast(FP8X4), scales=scales[:], in_=grouped[:])
+                w1_q[b][u] = (codes, scales)
+
+        got_w = [[None] * 2 for i in range(3)]
+
+        def gather_words(i, half):
+            g = keep.tile([P, HALF], U32, name=f"got_w{i}{half}", tag=f"got_w{i}{half}", align_bytes=64)
+            nc.vector.tensor_copy(g[:], tab_w[:].indirect(lists[i][:, 32 * half : 32 * (half + 1)]))
+            got_w[i][half] = g
+
+        def deal(name, raw, run):
+            words = raw.shape[1]
+            dealt = keep.tile([P, 4 * words], U8, name=name, tag=name, align_bytes=64)
+            nc.vector.tensor_copy(
+                out=dealt[:].bitcast(I32).rearrange("p (b t q e) -> p b t q e", b=2, t=4, e=run),
+                in_=raw.rearrange("p (b q t e) -> p b t q e", b=2, t=4, e=run),
+            )
+            return dealt
+
+        prepare_w1(0)
+        gain_ps = psum.tile([P, 2, 2 * P], F32, name="y_bank")
+        for b in range(2):
+            nc.tensor.transpose(gain_ps[:, b, 0:P], gain_rows[:, P * b : P * (b + 1)], ident[:])
+        gain_col = keep.tile([P, 2, 4], F32, name="gain_col")
+        nc.scalar.copy(out=gain_col[:], in_=gain_ps[:, :, 0:4])
+
+        w2_s = deal("w2_s", w2_sraw[:].bitcast(I32), 1)
+        gather_words(0, 0)
+        gather_words(1, 0)
+        w2_w = deal("w2_w", w2_raw[:], 2)
+        gather_words(2, 0)
+
+        w4_q = [None, None]
+
+        def prepare_w4(b):
+            grouped = ring.tile([P, 4 * N], BF16, name="w4_grouped", align_bytes=64, bufs=2)
+            dst = grouped[:].rearrange("p (s m t) -> p m t s", s=4, t=4)
+            src = w4_raw[b][:].rearrange("p t (m s) -> p m t s", s=4)
+            for u in range(4):
+                part = slice(32 * u, 32 * (u + 1))
+                if W4_ENG == "s":
+                    nc.scalar.copy(out=dst[:, part], in_=src[:, part])
+                elif W4_ENG == "g":
+                    nc.gpsimd.tensor_scalar(dst[:, part], src[:, part], 1.0, 0.0, ALU.mult, ALU.add)
+                else:
+                    nc.vector.tensor_copy(out=dst[:, part], in_=src[:, part])
+            codes = keep.tile([P, N], U32, name=f"w4_codes{b}", align_bytes=64)
+            scales = keep.tile([P, N], U8, name=f"w4_scales{b}", align_bytes=64)
+            nc.vector.quantize_mx(out=codes[:].bitcast(FP8X4), scales=scales[:], in_=grouped[:])
+            w4_q[b] = (codes, scales)
+
+        def moving(i, j0, width):
+            half, c0 = divmod(j0, HALF)
+            return got_w[i][half][:, c0 : c0 + width].bitcast(FP8X4), got_s[i][:, j0 : j0 + width]
+
+        gated = {}
+        h_q = {}
+
+        a_sb = {}
+        b_ps = {}
+        th = {}
+
+        def region(n):
+            k, u = divmod(n, 2)
+            b, jq = UNITS[k]
+            a_ps = psum.tile([P, 2 * W], F32, name="a_bank")
+            codes, scales = w1_q[b][u]
+            rhs, rhs_s = moving(0, W * jq, W)
+            for tt in range(2):
+                nc.tensor.matmul_mx(
+                    out=a_ps[:, W * tt : W * (tt + 1)], lhsT=codes[:, P * tt : P * (tt + 1)].bitcast(FP8X4),
+                    lhsT_scale=scales[:, P * tt : P * (tt + 1)], rhs=rhs, rhs_scale=rhs_s, start=True, stop=True,
+                )
+            if n in A_PIN:
+                a_sb[n] = keep.tile([P, 2 * W], F32, name=f"a_sb{n}", tag=A_PIN[n], align_bytes=64)
+            else:
+                a_sb[n] = ring.tile([P, 2 * W], F32, name="a_sb")
+            nc.scalar.copy(out=a_sb[n][:], in_=a_ps[:])
+
+        def gate(n):
+            k, u = divmod(n, 2)
+            b, jq = UNITS[k]
+            b_ps = psum.tile([P, 2 * W], F32, name="b_bank")
+            rhs, rhs_s = moving(1, W * jq, W)
+            for tt in range(2):
+                c0 = PASS * b + P * (2 * u + tt)
+                nc.tensor.matmul_mx(
+                    out=b_ps[:, W * tt : W * (tt + 1)], lhsT=w2_w[:, 2 * c0 : 2 * (c0 + P)].bitcast(FP4X4),
+                    lhsT_scale=w2_s[:, c0 : c0 + P], rhs=rhs, rhs_scale=rhs_s, start=True, stop=True,
+                )
+            if n >= AB_FROM:
+                ab = reuse.tile([P, 2 * W], F32, name=f"ab{n}", offset=8192 + 2048 * (n % 4))
+            else:
+                ab = ring.tile([P, 2 * W], F32, name="ab")
+            nc.vector.tensor_tensor(ab[:], a_sb[n][:], b_ps[:], ALU.mult)
+            if n >= TH_FROM:
+                th[n] = reuse.tile([P, 2 * W], F32, name=f"th{n}", offset=2048 * (n % 4))
+            else:
+                th[n] = ring.tile([P, 2 * W], F32, name="th")
+            nc.scalar.activation(out=th[n][:], in_=ab[:], func=ACT.Tanh)
+
+        def scale(n):
+            k, u = divmod(n, 2)
+            b, jq = UNITS[k]
+            if u == 0:
+                if k in W4_PIN:
+                    gated[k] = keep.tile([P, 4 * W], F32, name=f"gated{k}", tag=f"w4_raw{W4_PIN[k]}")
+                else:
+                    gated[k] = ring.tile([P, 4 * W], F32, name="gated")
+            for tt in range(2):
+                t = 2 * u + tt
+                dst = gated[k][:, W * t : W * (t + 1)]
+                src = th[n][:, W * tt : W * (tt + 1)]
+                g = gain_col[:, b, t : t + 1]
+                eng = GAIN_ENG[k][t]
+                if eng == "s":
+                    nc.scalar.activation(out=dst, in_=src, func=ACT.Copy, scale=g)
+                elif eng == "g":
+                    nc.gpsimd.tensor_scalar(dst, src, g, 0.0, ALU.mult, ALU.add)
+                else:
+                    nc.vector.tensor_scalar(dst, src, g, None, ALU.mult)
+
+        def join(k):
+            b, jq = UNITS[k]
+            grouped = ring.tile([P, 4 * W], BF16, name="h_grouped", align_bytes=64)
+            for v in range(2):
+                c_ps = psum.tile([P, 4 * P], F32, name="c_bank")
+                rhs, rhs_s = moving(2, W * jq + P * v, P)
+                for t in range(4):
+                    c0 = PASS * b + P * t
+                    nc.tensor.matmul_mx(
+                        out=c_ps[:, P * t : P * (t + 1)], lhsT=w3_w[:, 4 * c0 : 4 * (c0 + P)].bitcast(FP8X4),
+                        lhsT_scale=w3_s[:, c0 : c0 + P], rhs=rhs, rhs_scale=rhs_s, start=True, stop=True,
+                    )
+                nc.vector.tensor_tensor(
+                    grouped[:, 4 * P * v : 4 * P * (v + 1)].rearrange("p (c i t) -> p c t i", i=2, t=4),
+                    gated[k][:].rearrange("p (t v c i) -> p v c t i", t=4, v=2, i=2)[:, v],
+                    c_ps[:].rearrange("p (t c i) -> p c t i", t=4, i=2),
+                    ALU.add,
+                )
+            codes = keep.tile([P, W], U32, name=f"h_codes{k}", align_bytes=64)
+            scales = keep.tile([P, W], U8, name=f"h_scales{k}", align_bytes=64)
+            nc.vector.quantize_mx(out=codes[:].bitcast(FP8X4), scales=scales[:], in_=grouped[:])
+            h_q[(b, jq)] = (codes, scales)
+
+        y_scales = keep.tile([P, S], U8, name="y_scales", align_bytes=64)
+        out_rows = out_0.rearrange("(p s) j -> p s j", s=4)
+        out_words = out_1[0].rearrange("p m t -> p (m t)").bitcast(I32)
+
+        def answer(jq):
+            cols = slice(W * jq, W * (jq + 1))
+            y = ring.tile([P, 4 * W], F32, name="y", bufs=4)
+            for u in range(2):
+                y_ps = psum.tile([P, 2, W], F32, name="y_bank")
+                for ss in range(2):
+                    s = 2 * u + ss
+                    for b in range(2):
+                        codes, scales = w4_q[b]
+                        h_codes, h_scales = h_q[(b, jq)]
+                        nc.tensor.matmul_mx(
+                            out=y_ps[:, ss, :], lhsT=codes[:, P * s : P * (s + 1)].bitcast(FP8X4),
+                            lhsT_scale=scales[:, P * s : P * (s + 1)], rhs=h_codes[:].bitcast(FP8X4),
+                            rhs_scale=h_scales[:], start=(b == 0), stop=(b == 1),
+                        )
+                for ss in range(2):
+                    s = 2 * u + ss
+                    nc.scalar.activation(
+                        out=y[:, W * s : W * (s + 1)], in_=y_ps[:, ss, :], func=ACT.Identity, bias=bias_col[:, s : s + 1]
+                    )
+            nc.sync.dma_start(out=out_rows[:, :, cols], in_=y[:].rearrange("p (s j) -> p s j", s=4))
+            grouped = ring.tile([P, 4 * W], BF16, name="y_grouped", align_bytes=64)
+            dst = grouped[:].rearrange("p (c i s) -> p c s i", i=4, s=4)
+            src = y[:].rearrange("p (s c i) -> p c s i", s=4, i=4)
+            if YCAST_ENG[jq] == "s":
+                nc.scalar.copy(out=dst, in_=src)
+            else:
+                nc.vector.tensor_copy(out=dst, in_=src)
+            codes = keep.tile([P, W], U32, name=f"y_codes{jq}", align_bytes=64)
+            nc.vector.quantize_mx(out=codes[:].bitcast(FP8X4), scales=y_scales[:, cols], in_=grouped[:])
+            nc.sync.dma_start(out=out_words[:, cols], in_=codes[:].bitcast(I32))
+
+        region(0)
+        w3_w = deal("w3_w", w3_raw[:], 4)
+        region(1)
+        gate(0)
+        w3_s = deal("w3_s", w3_sraw[:].bitcast(I32), 1)
+        scale(0)
+        region(2)
+        gate(1)
+        scale(1)
+        region(3)
+        gate(2)
+        join(0)
+        gather_words(0, 1)
+        prepare_w1(1)
+        prepare_w4(0)
+        scale(2)
+        region(4)
+        gate(3)
+        scale(3)
+        region(5)
+        gate(4)
+        join(1)
+        gather_words(1, 1)
+        prepare_w4(1)
+        scale(4)
+        region(6)
+        gate(5)
+        scale(5)
+        region(7)
+        gate(6)
+        join(2)
+        gather_words(2, 1)
+        scale(6)
+        region(8)
+        gate(7)
+        scale(7)
+        answer(0)
+        region(9)
+        gate(8)
+        join(3)
+        scale(8)
+        region(10)
+        gate(9)
+        scale(9)
+        answer(1)
+        region(11)
+        gate(10)
+        join(4)
+        scale(10)
+        region(12)
+        gate(11)
+        scale(11)
+        region(13)
+        gate(12)
+        join(5)
+        scale(12)
+        answer(2)
+        region(14)
+        gate(13)
+        scale(13)
+        region(15)
+        gate(14)
+        join(6)
+        scale(14)
+        gate(15)
+        scale(15)
+        join(7)
+        answer(3)
+        for q in range(4):
+            queue = nc.sync if q % 2 == 0 else nc.scalar
+            queue.dma_start(
+                out=out_2[0, 4 * q : 4 * q + 4, :].bitcast(I32), in_=y_scales[32 * q : 32 * q + 4, :].bitcast(I32)
+            )

@@ -19,16 +19,11 @@ ALU = mybir.AluOpType
 P = 128
 PASS = 512
 HALF = 512
-W = 256
-UNITS = [(0, 0), (0, 1), (1, 0), (1, 1), (0, 2), (1, 2), (0, 3), (1, 3)]
-GAIN_ENG = ["gggg"] * 8
-YCAST_ENG = "vsvv"
-W4_PIN = {}
-A_PIN = {0: "w3_s", 2: "got_w01", 4: "got_w11", 6: "got_w21"}
+STEPS = [(0, 0), (0, 1), (0, 2), (0, 3), (1, 0), (1, 1), (1, 2), (1, 3), (0, 4), (0, 5), (1, 4), (1, 5), (0, 6), (0, 7), (1, 6), (1, 7)]
+GAIN_ENG = "G" * 16
+A_PIN = {0: "got_w20", 1: "w3_w", 3: "got_w01", 5: "got_w11", 7: "got_w21"}
+TH_PIN = {}
 W1_PIN = {(0, 0): "got_w00", (0, 1): "got_w10"}
-TH_FROM = 3
-AB_FROM = 5
-W4_ENG = "s"
 
 
 def tile_list_region_question_answer_kernel(
@@ -38,12 +33,14 @@ def tile_list_region_question_answer_kernel(
     nc = tc.nc
     with ExitStack() as ctx:
         keep = ctx.enter_context(tc.tile_pool(name="keep", bufs=1))
-        ring = ctx.enter_context(tc.tile_pool(name="ring", bufs=3))
+        ring = ctx.enter_context(tc.tile_pool(name="ring", bufs=2))
         psum = ctx.enter_context(tc.psum_pool(name="psum", bufs=2))
 
-        def load_scales(queue, plane, rows):
+        def load_scales(plane, rows):
             for q in range(4):
-                queue.dma_start(out=plane[32 * q : 32 * q + 4, :].bitcast(I32), in_=rows[0, 4 * q : 4 * q + 4, :].bitcast(I32))
+                nc.sync.dma_start(
+                    out=plane[32 * q : 32 * q + 4, :].bitcast(I32), in_=rows[0, 4 * q : 4 * q + 4, :].bitcast(I32)
+                )
 
         lists = []
         for i, src in enumerate((offs, offs2, offs3)):
@@ -52,7 +49,7 @@ def tile_list_region_question_answer_kernel(
             lists.append(lst)
         tab_s = keep.tile([P, T], U8, name="tab_s", align_bytes=64)
         nc.vector.memset(tab_s[:].bitcast(I32), 0)
-        load_scales(nc.sync, tab_s, tab_scales)
+        load_scales(tab_s, tab_scales)
         ident = keep.tile([P, P], F32, name="ident")
         with tc.tile_pool(name="setup", bufs=1) as setup:
             zeros = setup.tile([P, P], F32, name="zeros")
@@ -61,55 +58,77 @@ def tile_list_region_question_answer_kernel(
                 out=ident[:], in_=zeros[:], compare_op=ALU.not_equal, fill=1.0, base=0, pattern=[[-1, P]], channel_multiplier=1
             )
         stage = ctx.enter_context(tc.tile_pool(name="stage", bufs=1))
-        reuse = ctx.enter_context(tc.tile_pool(name="reuse", bufs=1))
 
         w1_raw = [stage.tile([P, 4, PASS], F32, name=f"w1_raw{b}") for b in range(2)]
         w1_rows = w1.rearrange("(p j) c -> p j c", j=4)
-        nc.sync.dma_start(out=w1_raw[0][:], in_=w1_rows[:, :, 0:PASS])
         tab_w = stage.tile([P, T], U32, name="tab_w", align_bytes=64)
-        nc.sync.dma_start(out=tab_w[:].bitcast(I32), in_=tab_words[0].rearrange("p n t -> p (n t)").bitcast(I32))
         w2_raw = stage.tile([P, H // 2], I32, name="w2_raw")
-        nc.sync.dma_start(out=w2_raw[:], in_=w2_words[0].bitcast(I32))
         gain_rows = stage.tile([P, 2 * P], F32, name="gain_rows")
-        nc.vector.memset(gain_rows[:], 0.0)
-        nc.sync.dma_start(
-            out=gain_rows[0:4, :].rearrange("t (g e) -> t g e", e=4),
-            in_=gain.rearrange("(g t e) -> t g e", t=4, e=4),
-        )
         w2_sraw = stage.tile([P, H], U8, name="w2_sraw")
-        nc.vector.memset(w2_sraw[:].bitcast(I32), 0)
-        load_scales(nc.sync, w2_sraw, w2_scales)
         w3_raw = stage.tile([P, H], I32, name="w3_raw")
-        nc.sync.dma_start(out=w3_raw[:], in_=w3_words[0].rearrange("p n t -> p (n t)").bitcast(I32))
         w3_sraw = stage.tile([P, H], U8, name="w3_sraw")
-        nc.vector.memset(w3_sraw[:].bitcast(I32), 0)
-        load_scales(nc.sync, w3_sraw, w3_scales)
-        nc.sync.dma_start(out=w1_raw[1][:], in_=w1_rows[:, :, PASS : 2 * PASS])
-        w4_raw = [reuse.tile([P, 4, N], F32, name=f"w4_raw{b}", offset=8192 * b) for b in range(2)]
-        for b in range(2):
-            rows = w4[PASS * b : PASS * (b + 1), :].rearrange("(q t e) n -> e q t n", t=4, e=4)
-            for e in range(4):
-                nc.sync.dma_start(out=w4_raw[b][e:P:4, :, :], in_=rows[e])
+        w4_raw = [stage.tile([P, 4, N], F32, name=f"w4_raw{b}") for b in range(2)]
         bias_col = stage.tile([P, 4], F32, name="bias_col")
-        nc.sync.dma_start(out=bias_col[:], in_=bias.rearrange("(p s) -> p s", s=4))
+        nc.vector.memset(gain_rows[:], 0.0)
+        nc.vector.memset(w2_sraw[:].bitcast(I32), 0)
+        nc.vector.memset(w3_sraw[:].bitcast(I32), 0)
 
+        def load_w1(b):
+            nc.sync.dma_start(out=w1_raw[b][:], in_=w1_rows[:, :, PASS * b : PASS * (b + 1)])
+
+        def load_w4(b):
+            rows = w4[PASS * b : PASS * (b + 1), :].rearrange("(q t e) n -> t q e n", t=4, e=4)
+            for t in range(4):
+                nc.sync.dma_start(out=w4_raw[b][:, t, :], in_=rows[t])
+
+        def load_table():
+            nc.sync.dma_start(out=tab_w[:].bitcast(I32), in_=tab_words[0].rearrange("p n t -> p (n t)").bitcast(I32))
+
+        def load_w2():
+            nc.sync.dma_start(out=w2_raw[:], in_=w2_words[0].bitcast(I32))
+
+        def load_gain():
+            nc.sync.dma_start(
+                out=gain_rows[0:4, :].rearrange("t (g e) -> t g e", e=4),
+                in_=gain.rearrange("(g t e) -> t g e", t=4, e=4),
+            )
+
+        def load_w3():
+            nc.sync.dma_start(out=w3_raw[:], in_=w3_words[0].rearrange("p n t -> p (n t)").bitcast(I32))
+
+        def load_bias():
+            nc.sync.dma_start(out=bias_col[:], in_=bias.rearrange("(p s) -> p s", s=4))
+
+        load_w1(0)
+        load_w1(1)
+        load_w2()
+        load_scales(w2_sraw, w2_scales)
+        load_table()
+        load_gain()
+        load_w3()
+        load_scales(w3_sraw, w3_scales)
+        load_w4(0)
+        load_w4(1)
+        load_bias()
 
         warm_in = keep.tile([P, 1], F32, name="warm_in")
         warm_out = keep.tile([P, 1], F32, name="warm_out")
         nc.vector.memset(warm_in[:], 0.0)
         nc.scalar.activation(out=warm_out[:], in_=warm_in[:], func=ACT.Tanh)
 
-        got_s = []
-        for i in range(3):
-            g = keep.tile([P, S], U8, name=f"got_s{i}", align_bytes=64)
-            nc.vector.tensor_copy(g[:], tab_s[:].indirect(lists[i][:]))
-            got_s.append(g)
+        got_s = [None] * 3
+
+        def gather_scales(i):
+            got_s[i] = keep.tile([P, S], U8, name=f"got_s{i}", align_bytes=64)
+            nc.vector.tensor_copy(got_s[i][:], tab_s[:].indirect(lists[i][:]))
 
         w1_q = [[None] * 2, [None] * 2]
 
         def prepare_w1(b):
             for u in range(2):
-                grouped = keep.tile([P, 1024], BF16, name=f"w1_grouped{b}{u}", tag=W1_PIN.get((b, u), f"w1_grouped{b}{u}"), align_bytes=64)
+                grouped = keep.tile(
+                    [P, 1024], BF16, name=f"w1_grouped{b}{u}", tag=W1_PIN.get((b, u), f"w1_grouped{b}{u}"), align_bytes=64
+                )
                 for tt in range(2):
                     t = 2 * u + tt
                     nc.scalar.copy(
@@ -137,102 +156,95 @@ def tile_list_region_question_answer_kernel(
             )
             return dealt
 
-        prepare_w1(0)
-        gain_ps = psum.tile([P, 2, 2 * P], F32, name="y_bank")
-        for b in range(2):
-            nc.tensor.transpose(gain_ps[:, b, 0:P], gain_rows[:, P * b : P * (b + 1)], ident[:])
         gain_col = keep.tile([P, 2, 4], F32, name="gain_col")
-        nc.scalar.copy(out=gain_col[:], in_=gain_ps[:, :, 0:4])
 
-        w2_s = deal("w2_s", w2_sraw[:].bitcast(I32), 1)
-        gather_words(0, 0)
-        gather_words(1, 0)
-        w2_w = deal("w2_w", w2_raw[:], 2)
-        gather_words(2, 0)
+        def spread_gain():
+            gain_ps = psum.tile([P, 2, 2 * P], F32, name="y_bank")
+            for b in range(2):
+                nc.tensor.transpose(gain_ps[:, b, 0:P], gain_rows[:, P * b : P * (b + 1)], ident[:])
+            nc.scalar.copy(out=gain_col[:], in_=gain_ps[:, :, 0:4])
 
         w4_q = [None, None]
+        w4_grouped = [keep.tile([P, 4 * N], BF16, name=f"w4_grouped{b}", align_bytes=64) for b in range(2)]
 
-        def prepare_w4(b):
-            grouped = ring.tile([P, 4 * N], BF16, name="w4_grouped", align_bytes=64, bufs=2)
-            dst = grouped[:].rearrange("p (s m t) -> p m t s", s=4, t=4)
+        def cast_w4(b, u, parts, eng):
+            dst = w4_grouped[b][:].rearrange("p (s m t) -> p m t s", s=4, t=4)
             src = w4_raw[b][:].rearrange("p t (m s) -> p m t s", s=4)
-            for u in range(4):
-                part = slice(32 * u, 32 * (u + 1))
-                if W4_ENG == "s":
-                    nc.scalar.copy(out=dst[:, part], in_=src[:, part])
-                elif W4_ENG == "g":
-                    nc.gpsimd.tensor_scalar(dst[:, part], src[:, part], 1.0, 0.0, ALU.mult, ALU.add)
-                else:
-                    nc.vector.tensor_copy(out=dst[:, part], in_=src[:, part])
+            part = slice(P // parts * u, P // parts * (u + 1))
+            if eng == "s":
+                nc.scalar.copy(out=dst[:, part], in_=src[:, part])
+            elif eng == "g":
+                nc.gpsimd.tensor_scalar(dst[:, part], src[:, part], 1.0, 0.0, ALU.mult, ALU.add)
+            else:
+                nc.vector.tensor_copy(out=dst[:, part], in_=src[:, part])
+
+        def quantise_w4(b):
             codes = keep.tile([P, N], U32, name=f"w4_codes{b}", align_bytes=64)
             scales = keep.tile([P, N], U8, name=f"w4_scales{b}", align_bytes=64)
-            nc.vector.quantize_mx(out=codes[:].bitcast(FP8X4), scales=scales[:], in_=grouped[:])
+            nc.vector.quantize_mx(out=codes[:].bitcast(FP8X4), scales=scales[:], in_=w4_grouped[b][:])
             w4_q[b] = (codes, scales)
 
-        def moving(i, j0, width):
-            half, c0 = divmod(j0, HALF)
-            return got_w[i][half][:, c0 : c0 + width].bitcast(FP8X4), got_s[i][:, j0 : j0 + width]
-
-        gated = {}
-        h_q = {}
+        def moving(i, c):
+            half, c0 = divmod(P * c, HALF)
+            return got_w[i][half][:, c0 : c0 + P].bitcast(FP8X4), got_s[i][:, P * c : P * (c + 1)]
 
         a_sb = {}
-        b_ps = {}
         th = {}
+        gated = {}
+        h_grouped = {}
+        h_q = {}
+        dealt = {}
 
         def region(n):
-            k, u = divmod(n, 2)
-            b, jq = UNITS[k]
-            a_ps = psum.tile([P, 2 * W], F32, name="a_bank")
-            codes, scales = w1_q[b][u]
-            rhs, rhs_s = moving(0, W * jq, W)
-            for tt in range(2):
+            b, c = STEPS[n]
+            a_ps = psum.tile([P, 4 * P], F32, name="a_bank")
+            rhs, rhs_s = moving(0, c)
+            for t in range(4):
+                codes, scales = w1_q[b][t // 2]
+                cols = slice(P * (t % 2), P * (t % 2 + 1))
                 nc.tensor.matmul_mx(
-                    out=a_ps[:, W * tt : W * (tt + 1)], lhsT=codes[:, P * tt : P * (tt + 1)].bitcast(FP8X4),
-                    lhsT_scale=scales[:, P * tt : P * (tt + 1)], rhs=rhs, rhs_scale=rhs_s, start=True, stop=True,
+                    out=a_ps[:, P * t : P * (t + 1)], lhsT=codes[:, cols].bitcast(FP8X4), lhsT_scale=scales[:, cols],
+                    rhs=rhs, rhs_scale=rhs_s, start=True, stop=True,
                 )
             if n in A_PIN:
-                a_sb[n] = keep.tile([P, 2 * W], F32, name=f"a_sb{n}", tag=A_PIN[n], align_bytes=64)
+                a_sb[n] = keep.tile([P, 4 * P], F32, name=f"a_sb{n}", tag=A_PIN[n], align_bytes=64)
             else:
-                a_sb[n] = ring.tile([P, 2 * W], F32, name="a_sb")
+                a_sb[n] = ring.tile([P, 4 * P], F32, name="a_sb", bufs=3)
             nc.scalar.copy(out=a_sb[n][:], in_=a_ps[:])
 
         def gate(n):
-            k, u = divmod(n, 2)
-            b, jq = UNITS[k]
-            b_ps = psum.tile([P, 2 * W], F32, name="b_bank")
-            rhs, rhs_s = moving(1, W * jq, W)
-            for tt in range(2):
-                c0 = PASS * b + P * (2 * u + tt)
+            b, c = STEPS[n]
+            b_ps = psum.tile([P, 4 * P], F32, name="b_bank")
+            rhs, rhs_s = moving(1, c)
+            for t in range(4):
+                c0 = PASS * b + P * t
                 nc.tensor.matmul_mx(
-                    out=b_ps[:, W * tt : W * (tt + 1)], lhsT=w2_w[:, 2 * c0 : 2 * (c0 + P)].bitcast(FP4X4),
-                    lhsT_scale=w2_s[:, c0 : c0 + P], rhs=rhs, rhs_scale=rhs_s, start=True, stop=True,
+                    out=b_ps[:, P * t : P * (t + 1)], lhsT=dealt["w2_w"][:, 2 * c0 : 2 * (c0 + P)].bitcast(FP4X4),
+                    lhsT_scale=dealt["w2_s"][:, c0 : c0 + P], rhs=rhs, rhs_scale=rhs_s, start=True, stop=True,
                 )
-            if n >= AB_FROM:
-                ab = reuse.tile([P, 2 * W], F32, name=f"ab{n}", offset=8192 + 2048 * (n % 4))
-            else:
-                ab = ring.tile([P, 2 * W], F32, name="ab")
+            ab = ring.tile([P, 4 * P], F32, name="ab")
             nc.vector.tensor_tensor(ab[:], a_sb[n][:], b_ps[:], ALU.mult)
-            if n >= TH_FROM:
-                th[n] = reuse.tile([P, 2 * W], F32, name=f"th{n}", offset=2048 * (n % 4))
+            if n in TH_PIN:
+                th[n] = keep.tile([P, 4 * P], F32, name=f"th{n}", tag=TH_PIN[n], align_bytes=64)
             else:
-                th[n] = ring.tile([P, 2 * W], F32, name="th")
+                th[n] = ring.tile([P, 4 * P], F32, name="th")
             nc.scalar.activation(out=th[n][:], in_=ab[:], func=ACT.Tanh)
 
         def scale(n):
-            k, u = divmod(n, 2)
-            b, jq = UNITS[k]
-            if u == 0:
-                if k in W4_PIN:
-                    gated[k] = keep.tile([P, 4 * W], F32, name=f"gated{k}", tag=f"w4_raw{W4_PIN[k]}")
-                else:
-                    gated[k] = ring.tile([P, 4 * W], F32, name="gated")
-            for tt in range(2):
-                t = 2 * u + tt
-                dst = gated[k][:, W * t : W * (t + 1)]
-                src = th[n][:, W * tt : W * (tt + 1)]
+            b, c = STEPS[n]
+            gated[n] = ring.tile([P, 4 * P], F32, name="gated")
+            eng = GAIN_ENG[n]
+            if eng in "GV":
+                engine = nc.gpsimd if eng == "G" else nc.vector
+                engine.tensor_tensor(
+                    gated[n][:].rearrange("p (t j) -> p t j", t=4), th[n][:].rearrange("p (t j) -> p t j", t=4),
+                    gain_col[:, b, :].unsqueeze(2).to_broadcast([P, 4, P]), ALU.mult,
+                )
+                return
+            for t in range(4):
+                dst = gated[n][:, P * t : P * (t + 1)]
+                src = th[n][:, P * t : P * (t + 1)]
                 g = gain_col[:, b, t : t + 1]
-                eng = GAIN_ENG[k][t]
                 if eng == "s":
                     nc.scalar.activation(out=dst, in_=src, func=ACT.Copy, scale=g)
                 elif eng == "g":
@@ -240,133 +252,186 @@ def tile_list_region_question_answer_kernel(
                 else:
                     nc.vector.tensor_scalar(dst, src, g, None, ALU.mult)
 
-        def join(k):
-            b, jq = UNITS[k]
-            grouped = ring.tile([P, 4 * W], BF16, name="h_grouped", align_bytes=64)
-            for v in range(2):
-                c_ps = psum.tile([P, 4 * P], F32, name="c_bank")
-                rhs, rhs_s = moving(2, W * jq + P * v, P)
-                for t in range(4):
-                    c0 = PASS * b + P * t
-                    nc.tensor.matmul_mx(
-                        out=c_ps[:, P * t : P * (t + 1)], lhsT=w3_w[:, 4 * c0 : 4 * (c0 + P)].bitcast(FP8X4),
-                        lhsT_scale=w3_s[:, c0 : c0 + P], rhs=rhs, rhs_scale=rhs_s, start=True, stop=True,
-                    )
-                nc.vector.tensor_tensor(
-                    grouped[:, 4 * P * v : 4 * P * (v + 1)].rearrange("p (c i t) -> p c t i", i=2, t=4),
-                    gated[k][:].rearrange("p (t v c i) -> p v c t i", t=4, v=2, i=2)[:, v],
-                    c_ps[:].rearrange("p (t c i) -> p c t i", t=4, i=2),
-                    ALU.add,
+        def join(n):
+            b, c = STEPS[n]
+            if c % 2 == 0:
+                h_grouped[b, c // 2] = keep.tile([P, 8 * P], BF16, name=f"h_grouped{n}", align_bytes=64)
+            c_ps = psum.tile([P, 4 * P], F32, name="c_bank")
+            rhs, rhs_s = moving(2, c)
+            for t in range(4):
+                c0 = PASS * b + P * t
+                nc.tensor.matmul_mx(
+                    out=c_ps[:, P * t : P * (t + 1)], lhsT=dealt["w3_w"][:, 4 * c0 : 4 * (c0 + P)].bitcast(FP8X4),
+                    lhsT_scale=dealt["w3_s"][:, c0 : c0 + P], rhs=rhs, rhs_scale=rhs_s, start=True, stop=True,
                 )
-            codes = keep.tile([P, W], U32, name=f"h_codes{k}", align_bytes=64)
-            scales = keep.tile([P, W], U8, name=f"h_scales{k}", align_bytes=64)
-            nc.vector.quantize_mx(out=codes[:].bitcast(FP8X4), scales=scales[:], in_=grouped[:])
-            h_q[(b, jq)] = (codes, scales)
+            nc.vector.tensor_tensor(
+                h_grouped[b, c // 2][:, 4 * P * (c % 2) : 4 * P * (c % 2 + 1)].rearrange("p (c i t) -> p c t i", i=2, t=4),
+                gated[n][:].rearrange("p (t c i) -> p c t i", t=4, i=2),
+                c_ps[:].rearrange("p (t c i) -> p c t i", t=4, i=2),
+                ALU.add,
+            )
+
+        def quantise_h(b, c, chunks):
+            width = P * chunks
+            codes = keep.tile([P, width], U32, name=f"h_codes{b}{c}", align_bytes=64)
+            scales = keep.tile([P, width], U8, name=f"h_scales{b}{c}", align_bytes=64)
+            first = 4 * P * (c % 2)
+            nc.vector.quantize_mx(
+                out=codes[:].bitcast(FP8X4), scales=scales[:], in_=h_grouped[b, c // 2][:, first : first + 4 * width]
+            )
+            for i in range(chunks):
+                h_q[b, c + i] = (codes, scales, P * i)
 
         y_scales = keep.tile([P, S], U8, name="y_scales", align_bytes=64)
         out_rows = out_0.rearrange("(p s) j -> p s j", s=4)
         out_words = out_1[0].rearrange("p m t -> p (m t)").bitcast(I32)
 
-        def answer(jq):
-            cols = slice(W * jq, W * (jq + 1))
-            y = ring.tile([P, 4 * W], F32, name="y", bufs=4)
-            for u in range(2):
-                y_ps = psum.tile([P, 2, W], F32, name="y_bank")
-                for ss in range(2):
-                    s = 2 * u + ss
+        def answer(c, chunks, evac, cast):
+            width = P * chunks
+            cols = slice(P * c, P * c + width)
+            y = keep.tile([P, 4 * width], F32, name=f"y{c}")
+            per_bank = 4 // chunks
+            for u in range(chunks):
+                y_ps = psum.tile([P, per_bank, width], F32, name="y_bank")
+                for ss in range(per_bank):
+                    s = per_bank * u + ss
                     for b in range(2):
                         codes, scales = w4_q[b]
-                        h_codes, h_scales = h_q[(b, jq)]
+                        h_codes, h_scales, h0 = h_q[b, c]
                         nc.tensor.matmul_mx(
                             out=y_ps[:, ss, :], lhsT=codes[:, P * s : P * (s + 1)].bitcast(FP8X4),
-                            lhsT_scale=scales[:, P * s : P * (s + 1)], rhs=h_codes[:].bitcast(FP8X4),
-                            rhs_scale=h_scales[:], start=(b == 0), stop=(b == 1),
+                            lhsT_scale=scales[:, P * s : P * (s + 1)], rhs=h_codes[:, h0 : h0 + width].bitcast(FP8X4),
+                            rhs_scale=h_scales[:, h0 : h0 + width], start=(b == 0), stop=(b == 1),
                         )
-                for ss in range(2):
-                    s = 2 * u + ss
-                    nc.scalar.activation(
-                        out=y[:, W * s : W * (s + 1)], in_=y_ps[:, ss, :], func=ACT.Identity, bias=bias_col[:, s : s + 1]
+                if evac[u] == "v":
+                    s0 = per_bank * u
+                    nc.vector.tensor_tensor(
+                        y[:, width * s0 : width * (s0 + per_bank)].rearrange("p (s j) -> p s j", s=per_bank), y_ps[:],
+                        bias_col[:, s0 : s0 + per_bank].unsqueeze(2).to_broadcast([P, per_bank, width]), ALU.add,
                     )
+                else:
+                    for ss in range(per_bank):
+                        s = per_bank * u + ss
+                        nc.scalar.activation(
+                            out=y[:, width * s : width * (s + 1)], in_=y_ps[:, ss, :], func=ACT.Identity,
+                            bias=bias_col[:, s : s + 1],
+                        )
             nc.sync.dma_start(out=out_rows[:, :, cols], in_=y[:].rearrange("p (s j) -> p s j", s=4))
-            grouped = ring.tile([P, 4 * W], BF16, name="y_grouped", align_bytes=64)
+            grouped = keep.tile([P, 4 * width], BF16, name=f"y_grouped{c}", align_bytes=64)
             dst = grouped[:].rearrange("p (c i s) -> p c s i", i=4, s=4)
             src = y[:].rearrange("p (s c i) -> p c s i", s=4, i=4)
-            if YCAST_ENG[jq] == "s":
+            if cast == "s":
                 nc.scalar.copy(out=dst, in_=src)
             else:
                 nc.vector.tensor_copy(out=dst, in_=src)
-            codes = keep.tile([P, W], U32, name=f"y_codes{jq}", align_bytes=64)
+            codes = keep.tile([P, width], U32, name=f"y_codes{c}", align_bytes=64)
             nc.vector.quantize_mx(out=codes[:].bitcast(FP8X4), scales=y_scales[:, cols], in_=grouped[:])
             nc.sync.dma_start(out=out_words[:, cols], in_=codes[:].bitcast(I32))
 
-        region(0)
-        w3_w = deal("w3_w", w3_raw[:], 4)
-        region(1)
-        gate(0)
-        w3_s = deal("w3_s", w3_sraw[:].bitcast(I32), 1)
-        scale(0)
-        region(2)
-        gate(1)
-        scale(1)
-        region(3)
-        gate(2)
-        join(0)
-        gather_words(0, 1)
+        gather_scales(0)
+        gather_scales(1)
+        gather_scales(2)
+        prepare_w1(0)
         prepare_w1(1)
-        prepare_w4(0)
-        scale(2)
+        dealt["w2_s"] = deal("w2_s", w2_sraw[:].bitcast(I32), 1)
+        dealt["w2_w"] = deal("w2_w", w2_raw[:], 2)
+        gather_words(0, 0)
+        gather_words(1, 0)
+        spread_gain()
+        region(0)
+        region(1)
+        region(2)
+        gate(0)
+        gather_words(2, 0)
+        scale(0)
+        region(3)
+        gate(1)
+        dealt["w3_w"] = deal("w3_w", w3_raw[:], 4)
+        dealt["w3_s"] = deal("w3_s", w3_sraw[:].bitcast(I32), 1)
+        scale(1)
         region(4)
-        gate(3)
-        scale(3)
+        gate(2)
+        scale(2)
+        join(0)
         region(5)
-        gate(4)
+        gate(3)
+        gather_words(0, 1)
+        scale(3)
         join(1)
-        gather_words(1, 1)
-        prepare_w4(1)
-        scale(4)
+        quantise_h(0, 0, 2)
+        cast_w4(0, 0, 4, "s")
+        cast_w4(0, 1, 4, "s")
+        cast_w4(0, 2, 4, "s")
+        cast_w4(0, 3, 4, "s")
+        quantise_w4(0)
+        cast_w4(1, 0, 4, "s")
+        cast_w4(1, 1, 4, "s")
+        cast_w4(1, 2, 4, "s")
+        cast_w4(1, 3, 4, "s")
+        quantise_w4(1)
         region(6)
-        gate(5)
-        scale(5)
-        region(7)
-        gate(6)
+        gate(4)
+        scale(4)
         join(2)
-        gather_words(2, 1)
-        scale(6)
-        region(8)
-        gate(7)
-        scale(7)
-        answer(0)
-        region(9)
-        gate(8)
+        region(7)
+        gate(5)
+        gather_words(1, 1)
+        scale(5)
         join(3)
-        scale(8)
+        quantise_h(0, 2, 2)
+        region(8)
+        gate(6)
+        scale(6)
+        join(4)
+        region(9)
+        gate(7)
+        gather_words(2, 1)
+        scale(7)
+        join(5)
+        quantise_h(1, 0, 2)
         region(10)
+        gate(8)
+        scale(8)
+        join(6)
+        region(11)
         gate(9)
         scale(9)
-        answer(1)
-        region(11)
-        gate(10)
-        join(4)
-        scale(10)
+        join(7)
+        quantise_h(1, 2, 2)
+        answer(0, 2, "ss", "v")
         region(12)
+        gate(10)
+        scale(10)
+        join(8)
+        region(13)
         gate(11)
         scale(11)
-        region(13)
-        gate(12)
-        join(5)
-        scale(12)
-        answer(2)
+        join(9)
+        quantise_h(0, 4, 2)
+        answer(2, 2, "ss", "v")
         region(14)
+        gate(12)
+        scale(12)
+        join(10)
+        region(15)
         gate(13)
         scale(13)
-        region(15)
+        join(11)
+        quantise_h(1, 4, 2)
         gate(14)
-        join(6)
         scale(14)
+        join(12)
+        answer(4, 2, "ss", "v")
         gate(15)
         scale(15)
-        join(7)
-        answer(3)
+        join(13)
+        quantise_h(0, 6, 2)
+        join(14)
+        quantise_h(1, 6, 1)
+        answer(6, 1, "s", "v")
+        join(15)
+        quantise_h(1, 7, 1)
+        answer(7, 1, "s", "v")
         for q in range(4):
             queue = nc.sync if q % 2 == 0 else nc.scalar
             queue.dma_start(

@@ -20,7 +20,7 @@ P = 128
 PASS = 512
 HALF = 512
 STEPS = [(0, 0), (0, 1), (0, 2), (0, 3), (1, 0), (1, 1), (1, 2), (1, 3), (0, 4), (0, 5), (1, 4), (1, 5), (0, 6), (0, 7), (1, 6), (1, 7)]
-GAIN_ENG = "G" * 16
+GAIN_ENG = ["sssv"] * 6 + ["ssvv"] * 10
 A_PIN = {0: "got_w20", 1: "w3_w", 3: "got_w01", 5: "got_w11", 7: "got_w21"}
 TH_PIN = {}
 W1_PIN = {(0, 0): "got_w00", (0, 1): "got_w10"}
@@ -33,7 +33,7 @@ def tile_list_region_question_answer_kernel(
     nc = tc.nc
     with ExitStack() as ctx:
         keep = ctx.enter_context(tc.tile_pool(name="keep", bufs=1))
-        ring = ctx.enter_context(tc.tile_pool(name="ring", bufs=2))
+        ring = ctx.enter_context(tc.tile_pool(name="ring", bufs=3))
         psum = ctx.enter_context(tc.psum_pool(name="psum", bufs=2))
 
         def load_scales(plane, rows):
@@ -209,7 +209,7 @@ def tile_list_region_question_answer_kernel(
             if n in A_PIN:
                 a_sb[n] = keep.tile([P, 4 * P], F32, name=f"a_sb{n}", tag=A_PIN[n], align_bytes=64)
             else:
-                a_sb[n] = ring.tile([P, 4 * P], F32, name="a_sb", bufs=3)
+                a_sb[n] = ring.tile([P, 4 * P], F32, name="a_sb", bufs=4)
             nc.scalar.copy(out=a_sb[n][:], in_=a_ps[:])
 
         def gate(n):
@@ -233,18 +233,11 @@ def tile_list_region_question_answer_kernel(
         def scale(n):
             b, c = STEPS[n]
             gated[n] = ring.tile([P, 4 * P], F32, name="gated")
-            eng = GAIN_ENG[n]
-            if eng in "GV":
-                engine = nc.gpsimd if eng == "G" else nc.vector
-                engine.tensor_tensor(
-                    gated[n][:].rearrange("p (t j) -> p t j", t=4), th[n][:].rearrange("p (t j) -> p t j", t=4),
-                    gain_col[:, b, :].unsqueeze(2).to_broadcast([P, 4, P]), ALU.mult,
-                )
-                return
             for t in range(4):
                 dst = gated[n][:, P * t : P * (t + 1)]
                 src = th[n][:, P * t : P * (t + 1)]
                 g = gain_col[:, b, t : t + 1]
+                eng = GAIN_ENG[n][t]
                 if eng == "s":
                     nc.scalar.activation(out=dst, in_=src, func=ACT.Copy, scale=g)
                 elif eng == "g":
@@ -341,24 +334,38 @@ def tile_list_region_question_answer_kernel(
         region(0)
         region(1)
         region(2)
+        region(3)
         gate(0)
         gather_words(2, 0)
         scale(0)
-        region(3)
+        region(4)
         gate(1)
         dealt["w3_w"] = deal("w3_w", w3_raw[:], 4)
         dealt["w3_s"] = deal("w3_s", w3_sraw[:].bitcast(I32), 1)
         scale(1)
-        region(4)
+        region(5)
         gate(2)
         scale(2)
-        join(0)
-        region(5)
+        region(6)
         gate(3)
         gather_words(0, 1)
         scale(3)
+        join(0)
+        region(7)
+        gate(4)
+        scale(4)
         join(1)
         quantise_h(0, 0, 2)
+        region(8)
+        gate(5)
+        gather_words(1, 1)
+        scale(5)
+        join(2)
+        region(9)
+        gate(6)
+        scale(6)
+        join(3)
+        quantise_h(0, 2, 2)
         cast_w4(0, 0, 4, "s")
         cast_w4(0, 1, 4, "s")
         cast_w4(0, 2, 4, "s")
@@ -369,61 +376,47 @@ def tile_list_region_question_answer_kernel(
         cast_w4(1, 2, 4, "s")
         cast_w4(1, 3, 4, "s")
         quantise_w4(1)
-        region(6)
-        gate(4)
-        scale(4)
-        join(2)
-        region(7)
-        gate(5)
-        gather_words(1, 1)
-        scale(5)
-        join(3)
-        quantise_h(0, 2, 2)
-        region(8)
-        gate(6)
-        scale(6)
-        join(4)
-        region(9)
+        region(10)
         gate(7)
         gather_words(2, 1)
         scale(7)
-        join(5)
-        quantise_h(1, 0, 2)
-        region(10)
+        join(4)
+        region(11)
         gate(8)
         scale(8)
-        join(6)
-        region(11)
+        join(5)
+        quantise_h(1, 0, 2)
+        region(12)
         gate(9)
         scale(9)
+        join(6)
+        region(13)
+        gate(10)
+        scale(10)
         join(7)
         quantise_h(1, 2, 2)
         answer(0, 2, "ss", "v")
-        region(12)
-        gate(10)
-        scale(10)
-        join(8)
-        region(13)
+        region(14)
         gate(11)
         scale(11)
+        join(8)
+        region(15)
+        gate(12)
+        scale(12)
         join(9)
         quantise_h(0, 4, 2)
         answer(2, 2, "ss", "v")
-        region(14)
-        gate(12)
-        scale(12)
-        join(10)
-        region(15)
         gate(13)
         scale(13)
-        join(11)
-        quantise_h(1, 4, 2)
+        join(10)
         gate(14)
         scale(14)
-        join(12)
-        answer(4, 2, "ss", "v")
+        join(11)
+        quantise_h(1, 4, 2)
         gate(15)
         scale(15)
+        join(12)
+        answer(4, 2, "ss", "v")
         join(13)
         quantise_h(0, 6, 2)
         join(14)

@@ -19,11 +19,15 @@ ALU = mybir.AluOpType
 P = 128
 PASS = 512
 HALF = 512
-STEPS = [(0, 0), (0, 1), (0, 2), (0, 3), (1, 0), (1, 1), (1, 2), (1, 3), (0, 4), (0, 5), (1, 4), (1, 5), (0, 6), (0, 7), (1, 6), (1, 7)]
-GAIN_ENG = ["sssv"] * 6 + ["ssvv"] * 10
-A_PIN = {0: "got_w20", 1: "w3_w", 3: "got_w01", 5: "got_w11", 7: "got_w21"}
+UNITS = [(0, 0), (0, 1), (1, 0), (1, 1), (0, 2), (1, 2), (0, 3), (1, 3)]
+W = 256
+H_SPAN = (4, 4, 2, 2)
+BY_COLUMNS = (7,)
+WHOLE_TANH = ()
+GAIN_ENG = ["gggg"] * 7 + ["ssss"]
+A_PIN = {1: "w3_w", 3: "got_w01", 5: "got_w11", 7: "got_w21"}
 TH_PIN = {}
-W1_PIN = {(0, 0): "got_w00", (0, 1): "got_w10"}
+W1_PIN = {0: "got_w00", 1: "got_w10"}
 
 
 def tile_list_region_question_answer_kernel(
@@ -122,23 +126,19 @@ def tile_list_region_question_answer_kernel(
             got_s[i] = keep.tile([P, S], U8, name=f"got_s{i}", align_bytes=64)
             nc.vector.tensor_copy(got_s[i][:], tab_s[:].indirect(lists[i][:]))
 
-        w1_q = [[None] * 2, [None] * 2]
+        w1_q = [None, None]
 
         def prepare_w1(b):
+            grouped = keep.tile([P, 4 * PASS], BF16, name=f"w1_grouped{b}", tag=W1_PIN.get(b, f"w1_grouped{b}"), align_bytes=64)
+            dst = grouped[:].rearrange("p (t q e j) -> p q t j e", t=4, e=4, j=4)
+            src = w1_raw[b][:].rearrange("p j (q t e) -> p q t j e", t=4, e=4)
             for u in range(2):
-                grouped = keep.tile(
-                    [P, 1024], BF16, name=f"w1_grouped{b}{u}", tag=W1_PIN.get((b, u), f"w1_grouped{b}{u}"), align_bytes=64
-                )
-                for tt in range(2):
-                    t = 2 * u + tt
-                    nc.scalar.copy(
-                        out=grouped[:, PASS * tt : PASS * (tt + 1)].rearrange("p (q e j) -> p q j e", e=4, j=4),
-                        in_=w1_raw[b][:].rearrange("p j (q t e) -> p t q j e", t=4, e=4)[:, t],
-                    )
-                codes = keep.tile([P, 2 * P], U32, name=f"w1_codes{b}{u}", align_bytes=64)
-                scales = keep.tile([P, 2 * P], U8, name=f"w1_scales{b}{u}", align_bytes=64)
-                nc.vector.quantize_mx(out=codes[:].bitcast(FP8X4), scales=scales[:], in_=grouped[:])
-                w1_q[b][u] = (codes, scales)
+                part = slice(32 // 2 * u, 32 // 2 * (u + 1))
+                nc.scalar.copy(out=dst[:, part], in_=src[:, part])
+            codes = keep.tile([P, PASS], U32, name=f"w1_codes{b}", align_bytes=64)
+            scales = keep.tile([P, PASS], U8, name=f"w1_scales{b}", align_bytes=64)
+            nc.vector.quantize_mx(out=codes[:].bitcast(FP8X4), scales=scales[:], in_=grouped[:])
+            w1_q[b] = (codes, scales)
 
         got_w = [[None] * 2 for i in range(3)]
 
@@ -184,11 +184,18 @@ def tile_list_region_question_answer_kernel(
             nc.vector.quantize_mx(out=codes[:].bitcast(FP8X4), scales=scales[:], in_=w4_grouped[b][:])
             w4_q[b] = (codes, scales)
 
-        def moving(i, c):
-            half, c0 = divmod(P * c, HALF)
-            return got_w[i][half][:, c0 : c0 + P].bitcast(FP8X4), got_s[i][:, P * c : P * (c + 1)]
+        def moving(i, j0, width):
+            half, c0 = divmod(j0, HALF)
+            return got_w[i][half][:, c0 : c0 + width].bitcast(FP8X4), got_s[i][:, j0 : j0 + width]
+
+        def blocks(n):
+            k, v = divmod(n, 2)
+            if k in BY_COLUMNS:
+                return [(t, P * v, P) for t in range(4)]
+            return [(2 * v, 0, W), (2 * v + 1, 0, W)]
 
         a_sb = {}
+        ab = {}
         th = {}
         gated = {}
         h_grouped = {}
@@ -196,48 +203,52 @@ def tile_list_region_question_answer_kernel(
         dealt = {}
 
         def region(n):
-            b, c = STEPS[n]
-            a_ps = psum.tile([P, 4 * P], F32, name="a_bank")
-            rhs, rhs_s = moving(0, c)
-            for t in range(4):
-                codes, scales = w1_q[b][t // 2]
-                cols = slice(P * (t % 2), P * (t % 2 + 1))
+            b, jq = UNITS[n // 2]
+            a_ps = psum.tile([P, 2 * W], F32, name="a_bank")
+            codes, scales = w1_q[b]
+            for i, (t, c0, width) in enumerate(blocks(n)):
+                rhs, rhs_s = moving(0, W * jq + c0, width)
+                cols = slice(P * t, P * (t + 1))
                 nc.tensor.matmul_mx(
-                    out=a_ps[:, P * t : P * (t + 1)], lhsT=codes[:, cols].bitcast(FP8X4), lhsT_scale=scales[:, cols],
+                    out=a_ps[:, width * i : width * (i + 1)], lhsT=codes[:, cols].bitcast(FP8X4), lhsT_scale=scales[:, cols],
                     rhs=rhs, rhs_scale=rhs_s, start=True, stop=True,
                 )
             if n in A_PIN:
-                a_sb[n] = keep.tile([P, 4 * P], F32, name=f"a_sb{n}", tag=A_PIN[n], align_bytes=64)
+                a_sb[n] = keep.tile([P, 2 * W], F32, name=f"a_sb{n}", tag=A_PIN[n], align_bytes=64)
             else:
-                a_sb[n] = ring.tile([P, 4 * P], F32, name="a_sb", bufs=4)
+                a_sb[n] = ring.tile([P, 2 * W], F32, name="a_sb", bufs=4)
             nc.scalar.copy(out=a_sb[n][:], in_=a_ps[:])
 
         def gate(n):
-            b, c = STEPS[n]
-            b_ps = psum.tile([P, 4 * P], F32, name="b_bank")
-            rhs, rhs_s = moving(1, c)
-            for t in range(4):
-                c0 = PASS * b + P * t
+            k, v = divmod(n, 2)
+            b, jq = UNITS[k]
+            b_ps = psum.tile([P, 2 * W], F32, name="b_bank")
+            for i, (t, c0, width) in enumerate(blocks(n)):
+                rhs, rhs_s = moving(1, W * jq + c0, width)
+                r0 = PASS * b + P * t
                 nc.tensor.matmul_mx(
-                    out=b_ps[:, P * t : P * (t + 1)], lhsT=dealt["w2_w"][:, 2 * c0 : 2 * (c0 + P)].bitcast(FP4X4),
-                    lhsT_scale=dealt["w2_s"][:, c0 : c0 + P], rhs=rhs, rhs_scale=rhs_s, start=True, stop=True,
+                    out=b_ps[:, width * i : width * (i + 1)], lhsT=dealt["w2_w"][:, 2 * r0 : 2 * (r0 + P)].bitcast(FP4X4),
+                    lhsT_scale=dealt["w2_s"][:, r0 : r0 + P], rhs=rhs, rhs_scale=rhs_s, start=True, stop=True,
                 )
-            ab = ring.tile([P, 4 * P], F32, name="ab")
-            nc.vector.tensor_tensor(ab[:], a_sb[n][:], b_ps[:], ALU.mult)
-            if n in TH_PIN:
-                th[n] = keep.tile([P, 4 * P], F32, name=f"th{n}", tag=TH_PIN[n], align_bytes=64)
-            else:
-                th[n] = ring.tile([P, 4 * P], F32, name="th")
-            nc.scalar.activation(out=th[n][:], in_=ab[:], func=ACT.Tanh)
+            if v == 0:
+                ab[k] = ring.tile([P, 4 * W], F32, name="ab", bufs=3)
+                th[k] = ring.tile([P, 4 * W], F32, name="th", bufs=3)
+                gated[k] = ring.tile([P, 4 * W], F32, name="gated", bufs=3)
+            half = slice(2 * W * v, 2 * W * (v + 1))
+            nc.vector.tensor_tensor(ab[k][:, half], a_sb[n][:], b_ps[:], ALU.mult)
+            if k not in WHOLE_TANH:
+                nc.scalar.activation(out=th[k][:, half], in_=ab[k][:, half], func=ACT.Tanh)
+            elif v == 1:
+                nc.scalar.activation(out=th[k][:], in_=ab[k][:], func=ACT.Tanh)
 
         def scale(n):
-            b, c = STEPS[n]
-            gated[n] = ring.tile([P, 4 * P], F32, name="gated")
-            for t in range(4):
-                dst = gated[n][:, P * t : P * (t + 1)]
-                src = th[n][:, P * t : P * (t + 1)]
+            k, v = divmod(n, 2)
+            b, jq = UNITS[k]
+            for i, (t, c0, width) in enumerate(blocks(n)):
+                dst = gated[k][:, W * t + c0 : W * t + c0 + width]
+                src = th[k][:, 2 * W * v + width * i : 2 * W * v + width * (i + 1)]
                 g = gain_col[:, b, t : t + 1]
-                eng = GAIN_ENG[n][t]
+                eng = GAIN_ENG[k][t]
                 if eng == "s":
                     nc.scalar.activation(out=dst, in_=src, func=ACT.Copy, scale=g)
                 elif eng == "g":
@@ -246,31 +257,36 @@ def tile_list_region_question_answer_kernel(
                     nc.vector.tensor_scalar(dst, src, g, None, ALU.mult)
 
         def join(n):
-            b, c = STEPS[n]
-            if c % 2 == 0:
-                h_grouped[b, c // 2] = keep.tile([P, 8 * P], BF16, name=f"h_grouped{n}", align_bytes=64)
+            k, v = divmod(n, 2)
+            b, jq = UNITS[k]
+            c = 2 * jq + v
+            span = H_SPAN[jq]
+            if c % span == 0:
+                h_grouped[b, c // span, span] = keep.tile([P, 4 * P * span], BF16, name=f"h_grouped{n}", align_bytes=64)
             c_ps = psum.tile([P, 4 * P], F32, name="c_bank")
-            rhs, rhs_s = moving(2, c)
+            rhs, rhs_s = moving(2, P * c, P)
             for t in range(4):
-                c0 = PASS * b + P * t
+                r0 = PASS * b + P * t
                 nc.tensor.matmul_mx(
-                    out=c_ps[:, P * t : P * (t + 1)], lhsT=dealt["w3_w"][:, 4 * c0 : 4 * (c0 + P)].bitcast(FP8X4),
-                    lhsT_scale=dealt["w3_s"][:, c0 : c0 + P], rhs=rhs, rhs_scale=rhs_s, start=True, stop=True,
+                    out=c_ps[:, P * t : P * (t + 1)], lhsT=dealt["w3_w"][:, 4 * r0 : 4 * (r0 + P)].bitcast(FP8X4),
+                    lhsT_scale=dealt["w3_s"][:, r0 : r0 + P], rhs=rhs, rhs_scale=rhs_s, start=True, stop=True,
                 )
+            first = 4 * P * (c % span)
             nc.vector.tensor_tensor(
-                h_grouped[b, c // 2][:, 4 * P * (c % 2) : 4 * P * (c % 2 + 1)].rearrange("p (c i t) -> p c t i", i=2, t=4),
-                gated[n][:].rearrange("p (t c i) -> p c t i", t=4, i=2),
+                h_grouped[b, c // span, span][:, first : first + 4 * P].rearrange("p (c i t) -> p c t i", i=2, t=4),
+                gated[k][:].rearrange("p (t v c i) -> p v c t i", t=4, v=2, i=2)[:, v],
                 c_ps[:].rearrange("p (t c i) -> p c t i", t=4, i=2),
                 ALU.add,
             )
 
         def quantise_h(b, c, chunks):
             width = P * chunks
+            span = H_SPAN[c // 2]
             codes = keep.tile([P, width], U32, name=f"h_codes{b}{c}", align_bytes=64)
             scales = keep.tile([P, width], U8, name=f"h_scales{b}{c}", align_bytes=64)
-            first = 4 * P * (c % 2)
+            first = 4 * P * (c % span)
             nc.vector.quantize_mx(
-                out=codes[:].bitcast(FP8X4), scales=scales[:], in_=h_grouped[b, c // 2][:, first : first + 4 * width]
+                out=codes[:].bitcast(FP8X4), scales=scales[:], in_=h_grouped[b, c // span, span][:, first : first + 4 * width]
             )
             for i in range(chunks):
                 h_q[b, c + i] = (codes, scales, P * i)
@@ -355,7 +371,6 @@ def tile_list_region_question_answer_kernel(
         gate(4)
         scale(4)
         join(1)
-        quantise_h(0, 0, 2)
         region(8)
         gate(5)
         gather_words(1, 1)
@@ -365,16 +380,12 @@ def tile_list_region_question_answer_kernel(
         gate(6)
         scale(6)
         join(3)
-        quantise_h(0, 2, 2)
-        cast_w4(0, 0, 4, "s")
-        cast_w4(0, 1, 4, "s")
-        cast_w4(0, 2, 4, "s")
-        cast_w4(0, 3, 4, "s")
+        quantise_h(0, 0, 4)
+        cast_w4(0, 0, 2, "s")
+        cast_w4(0, 1, 2, "s")
         quantise_w4(0)
-        cast_w4(1, 0, 4, "s")
-        cast_w4(1, 1, 4, "s")
-        cast_w4(1, 2, 4, "s")
-        cast_w4(1, 3, 4, "s")
+        cast_w4(1, 0, 2, "s")
+        cast_w4(1, 1, 2, "s")
         quantise_w4(1)
         region(10)
         gate(7)
@@ -385,7 +396,6 @@ def tile_list_region_question_answer_kernel(
         gate(8)
         scale(8)
         join(5)
-        quantise_h(1, 0, 2)
         region(12)
         gate(9)
         scale(9)
@@ -394,8 +404,7 @@ def tile_list_region_question_answer_kernel(
         gate(10)
         scale(10)
         join(7)
-        quantise_h(1, 2, 2)
-        answer(0, 2, "ss", "v")
+        quantise_h(1, 0, 4)
         region(14)
         gate(11)
         scale(11)
@@ -405,7 +414,7 @@ def tile_list_region_question_answer_kernel(
         scale(12)
         join(9)
         quantise_h(0, 4, 2)
-        answer(2, 2, "ss", "v")
+        answer(0, 4, "ssss", "v")
         gate(13)
         scale(13)
         join(10)

@@ -19,15 +19,13 @@ ALU = mybir.AluOpType
 P = 128
 PASS = 512
 HALF = 512
-UNITS = [(0, 0), (0, 1), (1, 0), (1, 1), (0, 2), (1, 2), (0, 3), (1, 3)]
-W = 256
-H_SPAN = (4, 4, 2, 2)
-BY_COLUMNS = (7,)
-WHOLE_TANH = ()
-GAIN_ENG = ["gggg"] * 7 + ["ssss"]
-A_PIN = {1: "w3_w", 3: "got_w01", 5: "got_w11", 7: "got_w21"}
-TH_PIN = {}
-W1_PIN = {0: "got_w00", 1: "got_w10"}
+CHUNKS = [(0, 512), (512, 512)]
+UNITS = [(c0, width, b) for c0, width in CHUNKS for b in range(2)]
+GAIN_ENG = ["gggg", "gggg", "gggg", "gggg"]
+BANKS = {"a": (0, 1, 2, 3, 4, 5, 6, 7), "b": (0, 1, 2, 3, 4, 5, 6, 7), "c": (0, 1, 2, 3), "y": (4, 5, 6, 7)}
+A_FIRST = ()
+GAIN_BANK = 7
+RUN = 2
 
 
 def tile_list_region_question_answer_kernel(
@@ -37,8 +35,20 @@ def tile_list_region_question_answer_kernel(
     nc = tc.nc
     with ExitStack() as ctx:
         keep = ctx.enter_context(tc.tile_pool(name="keep", bufs=1))
-        ring = ctx.enter_context(tc.tile_pool(name="ring", bufs=3))
-        psum = ctx.enter_context(tc.psum_pool(name="psum", bufs=2))
+        psum = ctx.enter_context(tc.psum_pool(name="psum", bufs=1))
+        used = {"a": [], "b": [], "c": [], "y": [], "g": []}
+
+        def bank(kind, shape):
+            n = len(used[kind])
+            used[kind].append(n)
+            if kind == "a" and n < len(A_FIRST):
+                place = A_FIRST[n]
+            elif kind == "g":
+                place = GAIN_BANK
+            else:
+                place = BANKS[kind][n % len(BANKS[kind])]
+            return psum.tile(shape, F32, name=f"{kind}_bank{n}", offset=2048 * place)
+
 
         def load_scales(plane, rows):
             for q in range(4):
@@ -105,12 +115,12 @@ def tile_list_region_question_answer_kernel(
 
         load_w1(0)
         load_w1(1)
+        load_table()
         load_w2()
         load_scales(w2_sraw, w2_scales)
-        load_table()
-        load_gain()
         load_w3()
         load_scales(w3_sraw, w3_scales)
+        load_gain()
         load_w4(0)
         load_w4(1)
         load_bias()
@@ -129,7 +139,7 @@ def tile_list_region_question_answer_kernel(
         w1_q = [None, None]
 
         def prepare_w1(b):
-            grouped = keep.tile([P, 4 * PASS], BF16, name=f"w1_grouped{b}", tag=W1_PIN.get(b, f"w1_grouped{b}"), align_bytes=64)
+            grouped = keep.tile([P, 4 * PASS], BF16, name=f"w1_grouped{b}", align_bytes=64)
             dst = grouped[:].rearrange("p (t q e j) -> p q t j e", t=4, e=4, j=4)
             src = w1_raw[b][:].rearrange("p j (q t e) -> p q t j e", t=4, e=4)
             for u in range(2):
@@ -143,7 +153,7 @@ def tile_list_region_question_answer_kernel(
         got_w = [[None] * 2 for i in range(3)]
 
         def gather_words(i, half):
-            g = keep.tile([P, HALF], U32, name=f"got_w{i}{half}", tag=f"got_w{i}{half}", align_bytes=64)
+            g = keep.tile([P, HALF], U32, name=f"got_w{i}{half}", align_bytes=64)
             nc.vector.tensor_copy(g[:], tab_w[:].indirect(lists[i][:, 32 * half : 32 * (half + 1)]))
             got_w[i][half] = g
 
@@ -159,7 +169,7 @@ def tile_list_region_question_answer_kernel(
         gain_col = keep.tile([P, 2, 4], F32, name="gain_col")
 
         def spread_gain():
-            gain_ps = psum.tile([P, 2, 2 * P], F32, name="y_bank")
+            gain_ps = bank("g", [P, 2, 2 * P])
             for b in range(2):
                 nc.tensor.transpose(gain_ps[:, b, 0:P], gain_rows[:, P * b : P * (b + 1)], ident[:])
             nc.scalar.copy(out=gain_col[:], in_=gain_ps[:, :, 0:4])
@@ -188,120 +198,106 @@ def tile_list_region_question_answer_kernel(
             half, c0 = divmod(j0, HALF)
             return got_w[i][half][:, c0 : c0 + width].bitcast(FP8X4), got_s[i][:, j0 : j0 + width]
 
-        def blocks(n):
-            k, v = divmod(n, 2)
-            if k in BY_COLUMNS:
-                return [(t, P * v, P) for t in range(4)]
-            return [(2 * v, 0, W), (2 * v + 1, 0, W)]
+        def steps(u):
+            width = UNITS[u][1]
+            per_bank = HALF // width
+            return [range(per_bank * n, per_bank * (n + 1)) for n in range(4 // per_bank)]
 
         a_sb = {}
-        ab = {}
-        th = {}
         gated = {}
         h_grouped = {}
         h_q = {}
         dealt = {}
 
-        def region(n):
-            b, jq = UNITS[n // 2]
-            a_ps = psum.tile([P, 2 * W], F32, name="a_bank")
+        def region(u):
+            c0, width, b = UNITS[u]
+            rhs, rhs_s = moving(0, c0, width)
             codes, scales = w1_q[b]
-            for i, (t, c0, width) in enumerate(blocks(n)):
-                rhs, rhs_s = moving(0, W * jq + c0, width)
-                cols = slice(P * t, P * (t + 1))
-                nc.tensor.matmul_mx(
-                    out=a_ps[:, width * i : width * (i + 1)], lhsT=codes[:, cols].bitcast(FP8X4), lhsT_scale=scales[:, cols],
-                    rhs=rhs, rhs_scale=rhs_s, start=True, stop=True,
-                )
-            if n in A_PIN:
-                a_sb[n] = keep.tile([P, 2 * W], F32, name=f"a_sb{n}", tag=A_PIN[n], align_bytes=64)
-            else:
-                a_sb[n] = ring.tile([P, 2 * W], F32, name="a_sb", bufs=4)
-            nc.scalar.copy(out=a_sb[n][:], in_=a_ps[:])
+            for n, slices in enumerate(steps(u)):
+                a_ps = bank("a", [P, HALF])
+                for i, t in enumerate(slices):
+                    cols = slice(P * t, P * (t + 1))
+                    nc.tensor.matmul_mx(
+                        out=a_ps[:, width * i : width * (i + 1)], lhsT=codes[:, cols].bitcast(FP8X4),
+                        lhsT_scale=scales[:, cols], rhs=rhs, rhs_scale=rhs_s, start=True, stop=True,
+                    )
+                a_sb[u, n] = keep.tile([P, HALF], F32, name=f"a_sb{u}{n}")
+                nc.scalar.copy(out=a_sb[u, n][:], in_=a_ps[:])
 
-        def gate(n):
-            k, v = divmod(n, 2)
-            b, jq = UNITS[k]
-            b_ps = psum.tile([P, 2 * W], F32, name="b_bank")
-            for i, (t, c0, width) in enumerate(blocks(n)):
-                rhs, rhs_s = moving(1, W * jq + c0, width)
-                r0 = PASS * b + P * t
-                nc.tensor.matmul_mx(
-                    out=b_ps[:, width * i : width * (i + 1)], lhsT=dealt["w2_w"][:, 2 * r0 : 2 * (r0 + P)].bitcast(FP4X4),
-                    lhsT_scale=dealt["w2_s"][:, r0 : r0 + P], rhs=rhs, rhs_scale=rhs_s, start=True, stop=True,
-                )
+        def gate(u):
+            c0, width, b = UNITS[u]
+            rhs, rhs_s = moving(1, c0, width)
+            gated[u] = keep.tile([P, 4 * width], F32, name=f"gated{u}")
+            for n, slices in enumerate(steps(u)):
+                b_ps = bank("b", [P, HALF])
+                for i, t in enumerate(slices):
+                    r0 = PASS * b + P * t
+                    nc.tensor.matmul_mx(
+                        out=b_ps[:, width * i : width * (i + 1)], lhsT=dealt["w2_w"][:, 2 * r0 : 2 * (r0 + P)].bitcast(FP4X4),
+                        lhsT_scale=dealt["w2_s"][:, r0 : r0 + P], rhs=rhs, rhs_scale=rhs_s, start=True, stop=True,
+                    )
+                ab = a_sb[u, n]
+                th = a_sb[u, n]
+                nc.vector.tensor_tensor(ab[:], a_sb[u, n][:], b_ps[:], ALU.mult)
+                nc.scalar.activation(out=th[:], in_=ab[:], func=ACT.Tanh)
+                for i, t in enumerate(slices):
+                    dst = gated[u][:, width * t : width * (t + 1)]
+                    src = th[:, width * i : width * (i + 1)]
+                    g = gain_col[:, b, t : t + 1]
+                    eng = GAIN_ENG[u][t]
+                    if eng == "s":
+                        nc.scalar.activation(out=dst, in_=src, func=ACT.Copy, scale=g)
+                    elif eng == "g":
+                        nc.gpsimd.tensor_scalar(dst, src, g, 0.0, ALU.mult, ALU.add)
+                    else:
+                        nc.vector.tensor_scalar(dst, src, g, None, ALU.mult)
+
+        def join(u, v):
+            c0, width, b = UNITS[u]
             if v == 0:
-                ab[k] = ring.tile([P, 4 * W], F32, name="ab", bufs=3)
-                th[k] = ring.tile([P, 4 * W], F32, name="th", bufs=3)
-                gated[k] = ring.tile([P, 4 * W], F32, name="gated", bufs=3)
-            half = slice(2 * W * v, 2 * W * (v + 1))
-            nc.vector.tensor_tensor(ab[k][:, half], a_sb[n][:], b_ps[:], ALU.mult)
-            if k not in WHOLE_TANH:
-                nc.scalar.activation(out=th[k][:, half], in_=ab[k][:, half], func=ACT.Tanh)
-            elif v == 1:
-                nc.scalar.activation(out=th[k][:], in_=ab[k][:], func=ACT.Tanh)
-
-        def scale(n):
-            k, v = divmod(n, 2)
-            b, jq = UNITS[k]
-            for i, (t, c0, width) in enumerate(blocks(n)):
-                dst = gated[k][:, W * t + c0 : W * t + c0 + width]
-                src = th[k][:, 2 * W * v + width * i : 2 * W * v + width * (i + 1)]
-                g = gain_col[:, b, t : t + 1]
-                eng = GAIN_ENG[k][t]
-                if eng == "s":
-                    nc.scalar.activation(out=dst, in_=src, func=ACT.Copy, scale=g)
-                elif eng == "g":
-                    nc.gpsimd.tensor_scalar(dst, src, g, 0.0, ALU.mult, ALU.add)
-                else:
-                    nc.vector.tensor_scalar(dst, src, g, None, ALU.mult)
-
-        def join(n):
-            k, v = divmod(n, 2)
-            b, jq = UNITS[k]
-            c = 2 * jq + v
-            span = H_SPAN[jq]
-            if c % span == 0:
-                h_grouped[b, c // span, span] = keep.tile([P, 4 * P * span], BF16, name=f"h_grouped{n}", align_bytes=64)
-            c_ps = psum.tile([P, 4 * P], F32, name="c_bank")
-            rhs, rhs_s = moving(2, P * c, P)
+                h_grouped[u] = keep.tile([P, 4 * width], BF16, name=f"h_grouped{u}", align_bytes=64)
+            c_ps = bank("c", [P, 4 * P])
+            rhs, rhs_s = moving(2, c0 + P * v, P)
             for t in range(4):
                 r0 = PASS * b + P * t
                 nc.tensor.matmul_mx(
                     out=c_ps[:, P * t : P * (t + 1)], lhsT=dealt["w3_w"][:, 4 * r0 : 4 * (r0 + P)].bitcast(FP8X4),
                     lhsT_scale=dealt["w3_s"][:, r0 : r0 + P], rhs=rhs, rhs_scale=rhs_s, start=True, stop=True,
                 )
-            first = 4 * P * (c % span)
             nc.vector.tensor_tensor(
-                h_grouped[b, c // span, span][:, first : first + 4 * P].rearrange("p (c i t) -> p c t i", i=2, t=4),
-                gated[k][:].rearrange("p (t v c i) -> p v c t i", t=4, v=2, i=2)[:, v],
-                c_ps[:].rearrange("p (t c i) -> p c t i", t=4, i=2),
+                h_grouped[u][:, 4 * P * v : 4 * P * (v + 1)].rearrange("p (c i t) -> p c t i", i=RUN, t=4),
+                gated[u][:].rearrange("p (t v c i) -> p v c t i", t=4, v=width // P, i=RUN)[:, v],
+                c_ps[:].rearrange("p (t c i) -> p c t i", t=4, i=RUN),
                 ALU.add,
             )
 
-        def quantise_h(b, c, chunks):
-            width = P * chunks
-            span = H_SPAN[c // 2]
-            codes = keep.tile([P, width], U32, name=f"h_codes{b}{c}", align_bytes=64)
-            scales = keep.tile([P, width], U8, name=f"h_scales{b}{c}", align_bytes=64)
-            first = 4 * P * (c % span)
+        def quantise_h(u, v, count):
+            c0, width, b = UNITS[u]
+            codes = keep.tile([P, P * count], U32, name=f"h_codes{u}{v}", align_bytes=64)
+            scales = keep.tile([P, P * count], U8, name=f"h_scales{u}{v}", align_bytes=64)
             nc.vector.quantize_mx(
-                out=codes[:].bitcast(FP8X4), scales=scales[:], in_=h_grouped[b, c // span, span][:, first : first + 4 * width]
+                out=codes[:].bitcast(FP8X4), scales=scales[:], in_=h_grouped[u][:, 4 * P * v : 4 * P * (v + count)]
             )
-            for i in range(chunks):
-                h_q[b, c + i] = (codes, scales, P * i)
+            for i in range(count):
+                h_q[b, c0 // P + v + i] = (codes, scales, P * i)
+
+        def join_all(u):
+            count = UNITS[u][1] // P
+            for v in range(count):
+                join(u, v)
+            quantise_h(u, 0, count)
 
         y_scales = keep.tile([P, S], U8, name="y_scales", align_bytes=64)
         out_rows = out_0.rearrange("(p s) j -> p s j", s=4)
         out_words = out_1[0].rearrange("p m t -> p (m t)").bitcast(I32)
+        y = {}
 
-        def answer(c, chunks, evac, cast):
+        def answer(c, chunks, evac):
             width = P * chunks
-            cols = slice(P * c, P * c + width)
-            y = keep.tile([P, 4 * width], F32, name=f"y{c}")
+            y[c] = keep.tile([P, 4 * width], F32, name=f"y{c}")
             per_bank = 4 // chunks
             for u in range(chunks):
-                y_ps = psum.tile([P, per_bank, width], F32, name="y_bank")
+                y_ps = bank("y", [P, per_bank, width])
                 for ss in range(per_bank):
                     s = per_bank * u + ss
                     for b in range(2):
@@ -312,29 +308,41 @@ def tile_list_region_question_answer_kernel(
                             lhsT_scale=scales[:, P * s : P * (s + 1)], rhs=h_codes[:, h0 : h0 + width].bitcast(FP8X4),
                             rhs_scale=h_scales[:, h0 : h0 + width], start=(b == 0), stop=(b == 1),
                         )
-                if evac[u] == "v":
+                if evac == "v":
                     s0 = per_bank * u
                     nc.vector.tensor_tensor(
-                        y[:, width * s0 : width * (s0 + per_bank)].rearrange("p (s j) -> p s j", s=per_bank), y_ps[:],
+                        y[c][:, width * s0 : width * (s0 + per_bank)].rearrange("p (s j) -> p s j", s=per_bank), y_ps[:],
                         bias_col[:, s0 : s0 + per_bank].unsqueeze(2).to_broadcast([P, per_bank, width]), ALU.add,
                     )
                 else:
                     for ss in range(per_bank):
                         s = per_bank * u + ss
                         nc.scalar.activation(
-                            out=y[:, width * s : width * (s + 1)], in_=y_ps[:, ss, :], func=ACT.Identity,
+                            out=y[c][:, width * s : width * (s + 1)], in_=y_ps[:, ss, :], func=ACT.Identity,
                             bias=bias_col[:, s : s + 1],
                         )
-            nc.sync.dma_start(out=out_rows[:, :, cols], in_=y[:].rearrange("p (s j) -> p s j", s=4))
-            grouped = keep.tile([P, 4 * width], BF16, name=f"y_grouped{c}", align_bytes=64)
-            dst = grouped[:].rearrange("p (c i s) -> p c s i", i=4, s=4)
-            src = y[:].rearrange("p (s c i) -> p c s i", s=4, i=4)
-            if cast == "s":
-                nc.scalar.copy(out=dst, in_=src)
-            else:
-                nc.vector.tensor_copy(out=dst, in_=src)
-            codes = keep.tile([P, width], U32, name=f"y_codes{c}", align_bytes=64)
-            nc.vector.quantize_mx(out=codes[:].bitcast(FP8X4), scales=y_scales[:, cols], in_=grouped[:])
+            nc.sync.dma_start(out=out_rows[:, :, P * c : P * c + width], in_=y[c][:].rearrange("p (s j) -> p s j", s=4))
+
+        y_grouped = {}
+
+        def round_y(c, chunks, cast):
+            y_grouped[c] = keep.tile([P, 4 * P * chunks], BF16, name=f"y_grouped{c}", align_bytes=64)
+            dst = y_grouped[c][:].rearrange("p (c i s) -> p c s i", i=4, s=4)
+            src = y[c][:].rearrange("p (s c i) -> p c s i", s=4, i=4)
+            size = 32 * chunks // len(cast)
+            for n, eng in enumerate(cast):
+                part = slice(size * n, size * (n + 1))
+                if eng == "s":
+                    nc.scalar.copy(out=dst[:, part], in_=src[:, part])
+                elif eng == "g":
+                    nc.gpsimd.tensor_scalar(dst[:, part], src[:, part], 1.0, 0.0, ALU.mult, ALU.add)
+                else:
+                    nc.vector.tensor_copy(out=dst[:, part], in_=src[:, part])
+
+        def planes(c, chunks):
+            cols = slice(P * c, P * (c + chunks))
+            codes = keep.tile([P, P * chunks], U32, name=f"y_codes{c}", align_bytes=64)
+            nc.vector.quantize_mx(out=codes[:].bitcast(FP8X4), scales=y_scales[:, cols], in_=y_grouped[c][:])
             nc.sync.dma_start(out=out_words[:, cols], in_=codes[:].bitcast(I32))
 
         gather_scales(0)
@@ -342,98 +350,50 @@ def tile_list_region_question_answer_kernel(
         gather_scales(2)
         prepare_w1(0)
         prepare_w1(1)
+        gather_words(0, 0)
+        gather_words(0, 1)
+        gather_words(1, 0)
         dealt["w2_s"] = deal("w2_s", w2_sraw[:].bitcast(I32), 1)
         dealt["w2_w"] = deal("w2_w", w2_raw[:], 2)
-        gather_words(0, 0)
-        gather_words(1, 0)
-        spread_gain()
+        dealt["w3_s"] = deal("w3_s", w3_sraw[:].bitcast(I32), 1)
+        dealt["w3_w"] = deal("w3_w", w3_raw[:], 4)
+        gather_words(1, 1)
+        gather_words(2, 0)
+        gather_words(2, 1)
         region(0)
         region(1)
+        spread_gain()
         region(2)
         region(3)
         gate(0)
-        gather_words(2, 0)
-        scale(0)
-        region(4)
         gate(1)
-        dealt["w3_w"] = deal("w3_w", w3_raw[:], 4)
-        dealt["w3_s"] = deal("w3_s", w3_sraw[:].bitcast(I32), 1)
-        scale(1)
-        region(5)
+        cast_w4(0, 0, 1, "s")
         gate(2)
-        scale(2)
-        region(6)
+        cast_w4(1, 0, 1, "s")
         gate(3)
-        gather_words(0, 1)
-        scale(3)
-        join(0)
-        region(7)
-        gate(4)
-        scale(4)
-        join(1)
-        region(8)
-        gate(5)
-        gather_words(1, 1)
-        scale(5)
-        join(2)
-        region(9)
-        gate(6)
-        scale(6)
-        join(3)
-        quantise_h(0, 0, 4)
-        cast_w4(0, 0, 2, "s")
-        cast_w4(0, 1, 2, "s")
+        join_all(0)
         quantise_w4(0)
-        cast_w4(1, 0, 2, "s")
-        cast_w4(1, 1, 2, "s")
+        for v in range(4):
+            join(1, v)
         quantise_w4(1)
-        region(10)
-        gate(7)
-        gather_words(2, 1)
-        scale(7)
-        join(4)
-        region(11)
-        gate(8)
-        scale(8)
-        join(5)
-        region(12)
-        gate(9)
-        scale(9)
-        join(6)
-        region(13)
-        gate(10)
-        scale(10)
-        join(7)
         quantise_h(1, 0, 4)
-        region(14)
-        gate(11)
-        scale(11)
-        join(8)
-        region(15)
-        gate(12)
-        scale(12)
-        join(9)
-        quantise_h(0, 4, 2)
-        answer(0, 4, "ssss", "v")
-        gate(13)
-        scale(13)
-        join(10)
-        gate(14)
-        scale(14)
-        join(11)
-        quantise_h(1, 4, 2)
-        gate(15)
-        scale(15)
-        join(12)
-        answer(4, 2, "ss", "v")
-        join(13)
-        quantise_h(0, 6, 2)
-        join(14)
-        quantise_h(1, 6, 1)
-        answer(6, 1, "s", "v")
-        join(15)
-        quantise_h(1, 7, 1)
-        answer(7, 1, "s", "v")
+        answer(0, 4, "s")
+        join_all(2)
+        join(3, 0)
+        join(3, 1)
+        quantise_h(3, 0, 2)
+        answer(4, 2, "s")
+        for v in (2, 3):
+            join(3, v)
+            quantise_h(3, v, 1)
+            answer(4 + v, 1, "s")
+        round_y(0, 4, "v")
+        planes(0, 4)
+        round_y(4, 2, "s")
+        planes(4, 2)
+        for v in range(2):
+            round_y(6 + v, 1, "v")
+            planes(6 + v, 1)
         for q in range(4):
             queue = nc.sync if q % 2 == 0 else nc.scalar
             queue.dma_start(

@@ -21,10 +21,12 @@ PASS = 512
 HALF = 512
 CHUNKS = [(0, 512), (512, 512)]
 UNITS = [(c0, width, b) for c0, width in CHUNKS for b in range(2)]
-GAIN_ENG = ["gggg", "gggg", "gggg", "gggg"]
-BANKS = {"a": (0, 1, 2, 3, 4, 5, 6, 7), "b": (0, 1, 2, 3, 4, 5, 6, 7), "c": (0, 1, 2, 3), "y": (4, 5, 6, 7)}
+GAIN_ENG = ["gggg", "gggg", "gggg", "ssss"]
+BANKS = {"a": (0, 1, 2, 3, 4, 5, 6, 7), "b": (0, 1, 2, 3, 4, 5, 6, 7), "c": (0, 1, 2, 3), "y": (4, 5, 6, 7), "z": (7, 0, 1, 2)}
 A_FIRST = ()
 GAIN_BANK = 7
+KB = 1024
+STAGING = 58 * KB
 RUN = 2
 
 
@@ -35,8 +37,9 @@ def tile_list_region_question_answer_kernel(
     nc = tc.nc
     with ExitStack() as ctx:
         keep = ctx.enter_context(tc.tile_pool(name="keep", bufs=1))
+        shared = ctx.enter_context(tc.tile_pool(name="shared", bufs=1))
         psum = ctx.enter_context(tc.psum_pool(name="psum", bufs=1))
-        used = {"a": [], "b": [], "c": [], "y": [], "g": []}
+        used = {"a": [], "b": [], "c": [], "y": [], "g": [], "z": []}
 
         def bank(kind, shape):
             n = len(used[kind])
@@ -50,9 +53,9 @@ def tile_list_region_question_answer_kernel(
             return psum.tile(shape, F32, name=f"{kind}_bank{n}", offset=2048 * place)
 
 
-        def load_scales(plane, rows):
+        def load_scales(plane, rows, queue=nc.sync):
             for q in range(4):
-                nc.sync.dma_start(
+                queue.dma_start(
                     out=plane[32 * q : 32 * q + 4, :].bitcast(I32), in_=rows[0, 4 * q : 4 * q + 4, :].bitcast(I32)
                 )
 
@@ -65,27 +68,24 @@ def tile_list_region_question_answer_kernel(
         nc.vector.memset(tab_s[:].bitcast(I32), 0)
         load_scales(tab_s, tab_scales)
         ident = keep.tile([P, P], F32, name="ident")
-        with tc.tile_pool(name="setup", bufs=1) as setup:
-            zeros = setup.tile([P, P], F32, name="zeros")
-            nc.vector.memset(zeros[:], 0.0)
-            nc.gpsimd.affine_select(
-                out=ident[:], in_=zeros[:], compare_op=ALU.not_equal, fill=1.0, base=0, pattern=[[-1, P]], channel_multiplier=1
-            )
-        stage = ctx.enter_context(tc.tile_pool(name="stage", bufs=1))
-
-        w1_raw = [stage.tile([P, 4, PASS], F32, name=f"w1_raw{b}") for b in range(2)]
+        zeros = shared.tile([P, STAGING // 4], F32, name="zeros", offset=0)
+        nc.vector.memset(zeros[:, 0:P], 0.0)
+        nc.gpsimd.affine_select(
+            out=ident[:], in_=zeros[:, 0:P], compare_op=ALU.not_equal, fill=1.0, base=0, pattern=[[-1, P]], channel_multiplier=1
+        )
+        tab_w = shared.tile([P, T], U32, name="tab_w", offset=0, align_bytes=64)
+        w3_raw = shared.tile([P, H], I32, name="w3_raw", offset=16 * KB)
+        w3_sraw = shared.tile([P, H], U8, name="w3_sraw", offset=20 * KB)
+        w2_raw = shared.tile([P, H // 2], I32, name="w2_raw", offset=21 * KB)
+        w2_sraw = shared.tile([P, H], U8, name="w2_sraw", offset=23 * KB)
+        w1_raw = [shared.tile([P, 4, PASS], F32, name=f"w1_raw{b}", offset=(24 + 8 * b) * KB) for b in range(2)]
+        w4_raw = [shared.tile([P, 4, N], F32, name=f"w4_raw{b}", offset=(40 + 8 * b) * KB) for b in range(2)]
+        gain_rows = shared.tile([P, 2 * P], F32, name="gain_rows", offset=56 * KB)
+        bias_col = shared.tile([P, 4], F32, name="bias_col", offset=57 * KB)
         w1_rows = w1.rearrange("(p j) c -> p j c", j=4)
-        tab_w = stage.tile([P, T], U32, name="tab_w", align_bytes=64)
-        w2_raw = stage.tile([P, H // 2], I32, name="w2_raw")
-        gain_rows = stage.tile([P, 2 * P], F32, name="gain_rows")
-        w2_sraw = stage.tile([P, H], U8, name="w2_sraw")
-        w3_raw = stage.tile([P, H], I32, name="w3_raw")
-        w3_sraw = stage.tile([P, H], U8, name="w3_sraw")
-        w4_raw = [stage.tile([P, 4, N], F32, name=f"w4_raw{b}") for b in range(2)]
-        bias_col = stage.tile([P, 4], F32, name="bias_col")
-        nc.vector.memset(gain_rows[:], 0.0)
         nc.vector.memset(w2_sraw[:].bitcast(I32), 0)
         nc.vector.memset(w3_sraw[:].bitcast(I32), 0)
+        nc.vector.memset(gain_rows[:], 0.0)
 
         def load_w1(b):
             nc.sync.dma_start(out=w1_raw[b][:], in_=w1_rows[:, :, PASS * b : PASS * (b + 1)])
@@ -119,10 +119,10 @@ def tile_list_region_question_answer_kernel(
         load_w2()
         load_scales(w2_sraw, w2_scales)
         load_w3()
-        load_scales(w3_sraw, w3_scales)
-        load_gain()
         load_w4(0)
         load_w4(1)
+        load_gain()
+        load_scales(w3_sraw, w3_scales)
         load_bias()
 
         warm_in = keep.tile([P, 1], F32, name="warm_in")
@@ -157,9 +157,12 @@ def tile_list_region_question_answer_kernel(
             nc.vector.tensor_copy(g[:], tab_w[:].indirect(lists[i][:, 32 * half : 32 * (half + 1)]))
             got_w[i][half] = g
 
-        def deal(name, raw, run):
+        def deal(name, raw, run, offset=None):
             words = raw.shape[1]
-            dealt = keep.tile([P, 4 * words], U8, name=name, tag=name, align_bytes=64)
+            if offset is None:
+                dealt = keep.tile([P, 4 * words], U8, name=name, align_bytes=64)
+            else:
+                dealt = shared.tile([P, 4 * words], U8, name=name, offset=offset, align_bytes=64)
             nc.vector.tensor_copy(
                 out=dealt[:].bitcast(I32).rearrange("p (b t q e) -> p b t q e", b=2, t=4, e=run),
                 in_=raw.rearrange("p (b q t e) -> p b t q e", b=2, t=4, e=run),
@@ -172,27 +175,36 @@ def tile_list_region_question_answer_kernel(
             gain_ps = bank("g", [P, 2, 2 * P])
             for b in range(2):
                 nc.tensor.transpose(gain_ps[:, b, 0:P], gain_rows[:, P * b : P * (b + 1)], ident[:])
-            nc.scalar.copy(out=gain_col[:], in_=gain_ps[:, :, 0:4])
+            nc.vector.tensor_copy(out=gain_col[:], in_=gain_ps[:, :, 0:4])
 
         w4_q = [None, None]
-        w4_grouped = [keep.tile([P, 4 * N], BF16, name=f"w4_grouped{b}", align_bytes=64) for b in range(2)]
+        w4_grouped = {}
 
         def cast_w4(b, u, parts, eng):
-            dst = w4_grouped[b][:].rearrange("p (s m t) -> p m t s", s=4, t=4)
+            if not w4_grouped:
+                both = shared.tile([P, 2 * 4 * N], BF16, name="w4_grouped", offset=12 * KB, align_bytes=64)
+                w4_grouped["both"] = both[:]
+                for i in range(2):
+                    w4_grouped[i] = both[:, 4 * N * i : 4 * N * (i + 1)]
+            dst = w4_grouped[b].rearrange("p (s m t) -> p m t s", s=4, t=4)
             src = w4_raw[b][:].rearrange("p t (m s) -> p m t s", s=4)
-            part = slice(P // parts * u, P // parts * (u + 1))
+            share = slice(4 // parts * u, 4 // parts * (u + 1))
             if eng == "s":
-                nc.scalar.copy(out=dst[:, part], in_=src[:, part])
+                nc.scalar.copy(out=dst[:, :, :, share], in_=src[:, :, :, share])
             elif eng == "g":
-                nc.gpsimd.tensor_scalar(dst[:, part], src[:, part], 1.0, 0.0, ALU.mult, ALU.add)
+                nc.gpsimd.tensor_scalar(
+                    w4_grouped[b].rearrange("p (s m t) -> p s m t", s=4, t=4)[:, share],
+                    w4_raw[b][:].rearrange("p t (m s) -> p s m t", s=4)[:, share], 1.0, 0.0, ALU.mult, ALU.add,
+                )
             else:
-                nc.vector.tensor_copy(out=dst[:, part], in_=src[:, part])
+                nc.vector.tensor_copy(out=dst[:, :, :, share], in_=src[:, :, :, share])
 
-        def quantise_w4(b):
-            codes = keep.tile([P, N], U32, name=f"w4_codes{b}", align_bytes=64)
-            scales = keep.tile([P, N], U8, name=f"w4_scales{b}", align_bytes=64)
-            nc.vector.quantize_mx(out=codes[:].bitcast(FP8X4), scales=scales[:], in_=w4_grouped[b][:])
-            w4_q[b] = (codes, scales)
+        def quantise_w4():
+            codes = keep.tile([P, 2 * N], U32, name="w4_codes", align_bytes=64)
+            scales = keep.tile([P, 2 * N], U8, name="w4_scales", align_bytes=64)
+            nc.vector.quantize_mx(out=codes[:].bitcast(FP8X4), scales=scales[:], in_=w4_grouped["both"])
+            for b in range(2):
+                w4_q[b] = (codes[:, N * b : N * (b + 1)], scales[:, N * b : N * (b + 1)])
 
         def moving(i, j0, width):
             half, c0 = divmod(j0, HALF)
@@ -252,52 +264,52 @@ def tile_list_region_question_answer_kernel(
                     else:
                         nc.vector.tensor_scalar(dst, src, g, None, ALU.mult)
 
-        def join(u, v):
-            c0, width, b = UNITS[u]
-            if v == 0:
-                h_grouped[u] = keep.tile([P, 4 * width], BF16, name=f"h_grouped{u}", align_bytes=64)
+        def join(c, b, first, chunks):
+            u = 2 * (P * c // HALF) + b
+            c0, width = UNITS[u][:2]
+            if c == first and b == 0:
+                h_grouped[first] = keep.tile([P, 2, 4 * P * chunks], BF16, name=f"h_grouped{first}", align_bytes=64)
             c_ps = bank("c", [P, 4 * P])
-            rhs, rhs_s = moving(2, c0 + P * v, P)
+            rhs, rhs_s = moving(2, P * c, P)
             for t in range(4):
                 r0 = PASS * b + P * t
                 nc.tensor.matmul_mx(
                     out=c_ps[:, P * t : P * (t + 1)], lhsT=dealt["w3_w"][:, 4 * r0 : 4 * (r0 + P)].bitcast(FP8X4),
                     lhsT_scale=dealt["w3_s"][:, r0 : r0 + P], rhs=rhs, rhs_scale=rhs_s, start=True, stop=True,
                 )
+            v = c - first
             nc.vector.tensor_tensor(
-                h_grouped[u][:, 4 * P * v : 4 * P * (v + 1)].rearrange("p (c i t) -> p c t i", i=RUN, t=4),
-                gated[u][:].rearrange("p (t v c i) -> p v c t i", t=4, v=width // P, i=RUN)[:, v],
+                h_grouped[first][:, b, 4 * P * v : 4 * P * (v + 1)].rearrange("p (c i t) -> p c t i", i=RUN, t=4),
+                gated[u][:].rearrange("p (t v c i) -> p v c t i", t=4, v=width // P, i=RUN)[:, c - c0 // P],
                 c_ps[:].rearrange("p (t c i) -> p c t i", t=4, i=RUN),
                 ALU.add,
             )
 
-        def quantise_h(u, v, count):
-            c0, width, b = UNITS[u]
-            codes = keep.tile([P, P * count], U32, name=f"h_codes{u}{v}", align_bytes=64)
-            scales = keep.tile([P, P * count], U8, name=f"h_scales{u}{v}", align_bytes=64)
-            nc.vector.quantize_mx(
-                out=codes[:].bitcast(FP8X4), scales=scales[:], in_=h_grouped[u][:, 4 * P * v : 4 * P * (v + count)]
-            )
-            for i in range(count):
-                h_q[b, c0 // P + v + i] = (codes, scales, P * i)
+        def join_piece(first, chunks):
+            for b in range(2):
+                for c in range(first, first + chunks):
+                    join(c, b, first, chunks)
 
-        def join_all(u):
-            count = UNITS[u][1] // P
-            for v in range(count):
-                join(u, v)
-            quantise_h(u, 0, count)
+        def quantise_h(first, chunks, halves):
+            width = P * chunks
+            count = len(halves)
+            codes = keep.tile([P, width * count], U32, name=f"h_codes{first}{halves[0]}", align_bytes=64)
+            scales = keep.tile([P, width * count], U8, name=f"h_scales{first}{halves[0]}", align_bytes=64)
+            src = h_grouped[first][:].rearrange("p b x -> p (b x)")[:, 4 * width * halves[0] : 4 * width * (halves[-1] + 1)]
+            nc.vector.quantize_mx(out=codes[:].bitcast(FP8X4), scales=scales[:], in_=src)
+            for i, b in enumerate(halves):
+                h_q[b, first] = (codes, scales, width * i)
 
         y_scales = keep.tile([P, S], U8, name="y_scales", align_bytes=64)
         out_rows = out_0.rearrange("(p s) j -> p s j", s=4)
         out_words = out_1[0].rearrange("p m t -> p (m t)").bitcast(I32)
         y = {}
 
-        def answer(c, chunks, evac):
+        def answer(c, chunks, evac, per_bank):
             width = P * chunks
             y[c] = keep.tile([P, 4 * width], F32, name=f"y{c}")
-            per_bank = 4 // chunks
-            for u in range(chunks):
-                y_ps = bank("y", [P, per_bank, width])
+            for u in range(4 // per_bank):
+                y_ps = bank("y" if per_bank * width == HALF else "z", [P, per_bank, width])
                 for ss in range(per_bank):
                     s = per_bank * u + ss
                     for b in range(2):
@@ -308,7 +320,7 @@ def tile_list_region_question_answer_kernel(
                             lhsT_scale=scales[:, P * s : P * (s + 1)], rhs=h_codes[:, h0 : h0 + width].bitcast(FP8X4),
                             rhs_scale=h_scales[:, h0 : h0 + width], start=(b == 0), stop=(b == 1),
                         )
-                if evac == "v":
+                if evac[u] == "v":
                     s0 = per_bank * u
                     nc.vector.tensor_tensor(
                         y[c][:, width * s0 : width * (s0 + per_bank)].rearrange("p (s j) -> p s j", s=per_bank), y_ps[:],
@@ -335,15 +347,23 @@ def tile_list_region_question_answer_kernel(
                 if eng == "s":
                     nc.scalar.copy(out=dst[:, part], in_=src[:, part])
                 elif eng == "g":
-                    nc.gpsimd.tensor_scalar(dst[:, part], src[:, part], 1.0, 0.0, ALU.mult, ALU.add)
+                    cols = slice(4 * size * n, 4 * size * (n + 1))
+                    nc.gpsimd.tensor_scalar(
+                        y_grouped[c][:].rearrange("p (j s) -> p j s", s=4)[:, cols],
+                        y[c][:].rearrange("p (s j) -> p j s", s=4)[:, cols], 1.0, 0.0, ALU.mult, ALU.add,
+                    )
                 else:
                     nc.vector.tensor_copy(out=dst[:, part], in_=src[:, part])
 
+        y_codes = keep.tile([P, S], U32, name="y_codes", align_bytes=64)
+
         def planes(c, chunks):
             cols = slice(P * c, P * (c + chunks))
-            codes = keep.tile([P, P * chunks], U32, name=f"y_codes{c}", align_bytes=64)
-            nc.vector.quantize_mx(out=codes[:].bitcast(FP8X4), scales=y_scales[:, cols], in_=y_grouped[c][:])
-            nc.sync.dma_start(out=out_words[:, cols], in_=codes[:].bitcast(I32))
+            nc.vector.quantize_mx(out=y_codes[:, cols].bitcast(FP8X4), scales=y_scales[:, cols], in_=y_grouped[c][:])
+
+        def store_words(c, chunks):
+            cols = slice(P * c, P * (c + chunks))
+            nc.sync.dma_start(out=out_words[:, cols], in_=y_codes[:, cols].bitcast(I32))
 
         gather_scales(0)
         gather_scales(1)
@@ -352,48 +372,59 @@ def tile_list_region_question_answer_kernel(
         prepare_w1(1)
         gather_words(0, 0)
         gather_words(0, 1)
-        gather_words(1, 0)
         dealt["w2_s"] = deal("w2_s", w2_sraw[:].bitcast(I32), 1)
-        dealt["w2_w"] = deal("w2_w", w2_raw[:], 2)
-        dealt["w3_s"] = deal("w3_s", w3_sraw[:].bitcast(I32), 1)
-        dealt["w3_w"] = deal("w3_w", w3_raw[:], 4)
+        gather_words(1, 0)
         gather_words(1, 1)
         gather_words(2, 0)
         gather_words(2, 1)
+        dealt["w2_w"] = deal("w2_w", w2_raw[:], 2, 0)
+        dealt["w3_w"] = deal("w3_w", w3_raw[:], 4, 23 * KB)
         region(0)
         region(1)
-        spread_gain()
         region(2)
         region(3)
+        spread_gain()
+        cast_w4(0, 0, 2, "g")
+        cast_w4(0, 1, 2, "g")
+        cast_w4(1, 0, 2, "g")
         gate(0)
         gate(1)
-        cast_w4(0, 0, 1, "s")
+        cast_w4(1, 1, 2, "s")
         gate(2)
-        cast_w4(1, 0, 1, "s")
+        dealt["w3_s"] = deal("w3_s", w3_sraw[:].bitcast(I32), 1)
         gate(3)
-        join_all(0)
-        quantise_w4(0)
-        for v in range(4):
-            join(1, v)
-        quantise_w4(1)
-        quantise_h(1, 0, 4)
-        answer(0, 4, "s")
-        join_all(2)
-        join(3, 0)
-        join(3, 1)
-        quantise_h(3, 0, 2)
-        answer(4, 2, "s")
-        for v in (2, 3):
-            join(3, v)
-            quantise_h(3, v, 1)
-            answer(4 + v, 1, "s")
-        round_y(0, 4, "v")
-        planes(0, 4)
-        round_y(4, 2, "s")
+        join_piece(0, 2)
+        join(2, 0, 2, 2)
+        join(3, 0, 2, 2)
+        quantise_w4()
+        quantise_h(0, 2, (0, 1))
+        answer(0, 2, "ss", 2)
+        round_y(0, 2, "s")
+        join(2, 1, 2, 2)
+        join(3, 1, 2, 2)
+        quantise_h(2, 2, (0, 1))
+        answer(2, 2, "ss", 2)
+        round_y(2, 2, "s")
+        join_piece(4, 2)
+        quantise_h(4, 2, (0, 1))
+        answer(4, 2, "ss", 2)
+        join_piece(6, 1)
+        quantise_h(6, 1, (0, 1))
+        answer(6, 1, "s", 4)
+        join(7, 0, 7, 1)
+        quantise_h(7, 1, (0,))
+        join(7, 1, 7, 1)
+        quantise_h(7, 1, (1,))
+        answer(7, 1, "ssss", 1)
+        planes(0, 2)
+        planes(2, 2)
+        round_y(4, 2, "v")
         planes(4, 2)
+        store_words(0, 6)
         for v in range(2):
             round_y(6 + v, 1, "v")
             planes(6 + v, 1)
+        store_words(6, 2)
         for q in range(4):
             queue = nc.sync if q % 2 == 0 else nc.scalar
             queue.dma_start(

@@ -21,12 +21,13 @@ PASS = 512
 HALF = 512
 CHUNKS = [(0, 512), (512, 512)]
 UNITS = [(c0, width, b) for c0, width in CHUNKS for b in range(2)]
-GAIN_ENG = ["gggg", "gggg", "gggg", "ssss"]
+GAIN_ENG = ["gggg", "gggg", "gggg", "ssgg"]
 BANKS = {"a": (0, 1, 2, 3, 4, 5, 6, 7), "b": (0, 1, 2, 3, 4, 5, 6, 7), "c": (0, 1, 2, 3), "y": (4, 5, 6, 7), "z": (7, 0, 1, 2)}
 A_FIRST = ()
 GAIN_BANK = 7
 KB = 1024
 STAGING = 58 * KB
+TANH_SPAN = (2, 2, 2, 2)
 RUN = 2
 
 
@@ -53,10 +54,10 @@ def tile_list_region_question_answer_kernel(
             return psum.tile(shape, F32, name=f"{kind}_bank{n}", offset=2048 * place)
 
 
-        def load_scales(plane, rows, queue=nc.sync):
+        def load_scales(plane, rows, first=0):
             for q in range(4):
-                queue.dma_start(
-                    out=plane[32 * q : 32 * q + 4, :].bitcast(I32), in_=rows[0, 4 * q : 4 * q + 4, :].bitcast(I32)
+                nc.sync.dma_start(
+                    out=plane[32 * q + first : 32 * q + first + 4, :].bitcast(I32), in_=rows[0, 4 * q : 4 * q + 4, :].bitcast(I32)
                 )
 
         lists = []
@@ -75,16 +76,14 @@ def tile_list_region_question_answer_kernel(
         )
         tab_w = shared.tile([P, T], U32, name="tab_w", offset=0, align_bytes=64)
         w3_raw = shared.tile([P, H], I32, name="w3_raw", offset=16 * KB)
-        w3_sraw = shared.tile([P, H], U8, name="w3_sraw", offset=20 * KB)
         w2_raw = shared.tile([P, H // 2], I32, name="w2_raw", offset=21 * KB)
-        w2_sraw = shared.tile([P, H], U8, name="w2_sraw", offset=23 * KB)
+        w_sraw = shared.tile([P, H], U8, name="w_sraw", offset=23 * KB)
         w1_raw = [shared.tile([P, 4, PASS], F32, name=f"w1_raw{b}", offset=(24 + 8 * b) * KB) for b in range(2)]
         w4_raw = [shared.tile([P, 4, N], F32, name=f"w4_raw{b}", offset=(40 + 8 * b) * KB) for b in range(2)]
         gain_rows = shared.tile([P, 2 * P], F32, name="gain_rows", offset=56 * KB)
         bias_col = shared.tile([P, 4], F32, name="bias_col", offset=57 * KB)
         w1_rows = w1.rearrange("(p j) c -> p j c", j=4)
-        nc.vector.memset(w2_sraw[:].bitcast(I32), 0)
-        nc.vector.memset(w3_sraw[:].bitcast(I32), 0)
+        nc.vector.memset(w_sraw[:].bitcast(I32), 0)
         nc.vector.memset(gain_rows[:], 0.0)
 
         def load_w1(b):
@@ -117,12 +116,12 @@ def tile_list_region_question_answer_kernel(
         load_w1(1)
         load_table()
         load_w2()
-        load_scales(w2_sraw, w2_scales)
         load_w3()
+        load_scales(w_sraw, w2_scales)
+        load_scales(w_sraw, w3_scales, 4)
+        load_gain()
         load_w4(0)
         load_w4(1)
-        load_gain()
-        load_scales(w3_sraw, w3_scales)
         load_bias()
 
         warm_in = keep.tile([P, 1], F32, name="warm_in")
@@ -155,7 +154,13 @@ def tile_list_region_question_answer_kernel(
         def gather_words(i, half):
             g = keep.tile([P, HALF], U32, name=f"got_w{i}{half}", align_bytes=64)
             nc.vector.tensor_copy(g[:], tab_w[:].indirect(lists[i][:, 32 * half : 32 * (half + 1)]))
-            got_w[i][half] = g
+            got_w[i][half] = g[:]
+
+        def gather_list(i):
+            g = keep.tile([P, S], U32, name=f"got_w{i}", align_bytes=64)
+            nc.vector.tensor_copy(g[:], tab_w[:].indirect(lists[i][:]))
+            for half in range(2):
+                got_w[i][half] = g[:, HALF * half : HALF * (half + 1)]
 
         def deal(name, raw, run, offset=None):
             words = raw.shape[1]
@@ -175,14 +180,14 @@ def tile_list_region_question_answer_kernel(
             gain_ps = bank("g", [P, 2, 2 * P])
             for b in range(2):
                 nc.tensor.transpose(gain_ps[:, b, 0:P], gain_rows[:, P * b : P * (b + 1)], ident[:])
-            nc.vector.tensor_copy(out=gain_col[:], in_=gain_ps[:, :, 0:4])
+            nc.scalar.copy(out=gain_col[:], in_=gain_ps[:, :, 0:4])
 
         w4_q = [None, None]
         w4_grouped = {}
 
         def cast_w4(b, u, parts, eng):
             if not w4_grouped:
-                both = shared.tile([P, 2 * 4 * N], BF16, name="w4_grouped", offset=12 * KB, align_bytes=64)
+                both = shared.tile([P, 2 * 4 * N], BF16, name="w4_grouped", offset=32 * KB, align_bytes=64)
                 w4_grouped["both"] = both[:]
                 for i in range(2):
                     w4_grouped[i] = both[:, 4 * N * i : 4 * N * (i + 1)]
@@ -233,8 +238,9 @@ def tile_list_region_question_answer_kernel(
                         out=a_ps[:, width * i : width * (i + 1)], lhsT=codes[:, cols].bitcast(FP8X4),
                         lhsT_scale=scales[:, cols], rhs=rhs, rhs_scale=rhs_s, start=True, stop=True,
                     )
-                a_sb[u, n] = keep.tile([P, HALF], F32, name=f"a_sb{u}{n}")
-                nc.scalar.copy(out=a_sb[u, n][:], in_=a_ps[:])
+                if n == 0:
+                    a_sb[u] = keep.tile([P, 4 * width], F32, name=f"a_sb{u}")
+                nc.scalar.copy(out=a_sb[u][:, HALF * n : HALF * (n + 1)], in_=a_ps[:])
 
         def gate(u):
             c0, width, b = UNITS[u]
@@ -246,40 +252,39 @@ def tile_list_region_question_answer_kernel(
                     r0 = PASS * b + P * t
                     nc.tensor.matmul_mx(
                         out=b_ps[:, width * i : width * (i + 1)], lhsT=dealt["w2_w"][:, 2 * r0 : 2 * (r0 + P)].bitcast(FP4X4),
-                        lhsT_scale=dealt["w2_s"][:, r0 : r0 + P], rhs=rhs, rhs_scale=rhs_s, start=True, stop=True,
+                        lhsT_scale=dealt["w_s"][:, r0 : r0 + P], rhs=rhs, rhs_scale=rhs_s, start=True, stop=True,
                     )
-                ab = a_sb[u, n]
-                th = a_sb[u, n]
-                nc.vector.tensor_tensor(ab[:], a_sb[u, n][:], b_ps[:], ALU.mult)
-                nc.scalar.activation(out=th[:], in_=ab[:], func=ACT.Tanh)
-                for i, t in enumerate(slices):
-                    dst = gated[u][:, width * t : width * (t + 1)]
-                    src = th[:, width * i : width * (i + 1)]
-                    g = gain_col[:, b, t : t + 1]
-                    eng = GAIN_ENG[u][t]
-                    if eng == "s":
-                        nc.scalar.activation(out=dst, in_=src, func=ACT.Copy, scale=g)
-                    elif eng == "g":
-                        nc.gpsimd.tensor_scalar(dst, src, g, 0.0, ALU.mult, ALU.add)
-                    else:
-                        nc.vector.tensor_scalar(dst, src, g, None, ALU.mult)
+                ab = a_sb[u][:, HALF * n : HALF * (n + 1)]
+                nc.vector.tensor_tensor(ab, ab, b_ps[:], ALU.mult)
+                span = TANH_SPAN[u]
+                if (n + 1) % span == 0:
+                    th = a_sb[u][:, HALF * (n + 1 - span) : HALF * (n + 1)]
+                    nc.scalar.activation(out=th, in_=th, func=ACT.Tanh)
+                    for t in range(n + 1 - span, n + 1):
+                        dst = gated[u][:, width * t : width * (t + 1)]
+                        src = a_sb[u][:, width * t : width * (t + 1)]
+                        g = gain_col[:, b, t : t + 1]
+                        if GAIN_ENG[u][t] == "s":
+                            nc.scalar.activation(out=dst, in_=src, func=ACT.Copy, scale=g)
+                        else:
+                            nc.gpsimd.tensor_scalar(dst, src, g, 0.0, ALU.mult, ALU.add)
 
         def join(c, b, first, chunks):
             u = 2 * (P * c // HALF) + b
             c0, width = UNITS[u][:2]
             if c == first and b == 0:
-                h_grouped[first] = keep.tile([P, 2, 4 * P * chunks], BF16, name=f"h_grouped{first}", align_bytes=64)
+                h_grouped[first] = keep.tile([P, 2 * 4 * P * chunks], BF16, name=f"h_grouped{first}", align_bytes=64)
             c_ps = bank("c", [P, 4 * P])
             rhs, rhs_s = moving(2, P * c, P)
             for t in range(4):
                 r0 = PASS * b + P * t
                 nc.tensor.matmul_mx(
                     out=c_ps[:, P * t : P * (t + 1)], lhsT=dealt["w3_w"][:, 4 * r0 : 4 * (r0 + P)].bitcast(FP8X4),
-                    lhsT_scale=dealt["w3_s"][:, r0 : r0 + P], rhs=rhs, rhs_scale=rhs_s, start=True, stop=True,
+                    lhsT_scale=dealt["w_s"][4:P, r0 : r0 + P], rhs=rhs, rhs_scale=rhs_s, start=True, stop=True,
                 )
-            v = c - first
+            v = b * chunks + c - first
             nc.vector.tensor_tensor(
-                h_grouped[first][:, b, 4 * P * v : 4 * P * (v + 1)].rearrange("p (c i t) -> p c t i", i=RUN, t=4),
+                h_grouped[first][:, 4 * P * v : 4 * P * (v + 1)].rearrange("p (c i t) -> p c t i", i=RUN, t=4),
                 gated[u][:].rearrange("p (t v c i) -> p v c t i", t=4, v=width // P, i=RUN)[:, c - c0 // P],
                 c_ps[:].rearrange("p (t c i) -> p c t i", t=4, i=RUN),
                 ALU.add,
@@ -295,7 +300,7 @@ def tile_list_region_question_answer_kernel(
             count = len(halves)
             codes = keep.tile([P, width * count], U32, name=f"h_codes{first}{halves[0]}", align_bytes=64)
             scales = keep.tile([P, width * count], U8, name=f"h_scales{first}{halves[0]}", align_bytes=64)
-            src = h_grouped[first][:].rearrange("p b x -> p (b x)")[:, 4 * width * halves[0] : 4 * width * (halves[-1] + 1)]
+            src = h_grouped[first][:, 4 * width * halves[0] : 4 * width * (halves[-1] + 1)]
             nc.vector.quantize_mx(out=codes[:].bitcast(FP8X4), scales=scales[:], in_=src)
             for i, b in enumerate(halves):
                 h_q[b, first] = (codes, scales, width * i)
@@ -372,58 +377,50 @@ def tile_list_region_question_answer_kernel(
         prepare_w1(1)
         gather_words(0, 0)
         gather_words(0, 1)
-        dealt["w2_s"] = deal("w2_s", w2_sraw[:].bitcast(I32), 1)
-        gather_words(1, 0)
-        gather_words(1, 1)
-        gather_words(2, 0)
-        gather_words(2, 1)
+        gather_list(1)
+        gather_list(2)
         dealt["w2_w"] = deal("w2_w", w2_raw[:], 2, 0)
+        dealt["w_s"] = deal("w_s", w_sraw[:].bitcast(I32), 1)
         dealt["w3_w"] = deal("w3_w", w3_raw[:], 4, 23 * KB)
         region(0)
         region(1)
+        spread_gain()
         region(2)
         region(3)
-        spread_gain()
-        cast_w4(0, 0, 2, "g")
-        cast_w4(0, 1, 2, "g")
-        cast_w4(1, 0, 2, "g")
         gate(0)
         gate(1)
-        cast_w4(1, 1, 2, "s")
+        cast_w4(0, 0, 1, "s")
         gate(2)
-        dealt["w3_s"] = deal("w3_s", w3_sraw[:].bitcast(I32), 1)
+        cast_w4(1, 0, 1, "s")
         gate(3)
-        join_piece(0, 2)
-        join(2, 0, 2, 2)
-        join(3, 0, 2, 2)
+        join_piece(0, 4)
         quantise_w4()
-        quantise_h(0, 2, (0, 1))
-        answer(0, 2, "ss", 2)
-        round_y(0, 2, "s")
-        join(2, 1, 2, 2)
-        join(3, 1, 2, 2)
-        quantise_h(2, 2, (0, 1))
-        answer(2, 2, "ss", 2)
-        round_y(2, 2, "s")
-        join_piece(4, 2)
+        quantise_h(0, 4, (0, 1))
+        answer(0, 4, "ssss", 1)
+        round_y(0, 4, "ss")
+        join(4, 0, 4, 2)
+        join(5, 0, 4, 2)
+        join(6, 0, 6, 1)
+        join(4, 1, 4, 2)
+        join(5, 1, 4, 2)
+        join(7, 0, 7, 1)
         quantise_h(4, 2, (0, 1))
         answer(4, 2, "ss", 2)
-        join_piece(6, 1)
-        quantise_h(6, 1, (0, 1))
-        answer(6, 1, "s", 4)
-        join(7, 0, 7, 1)
+        join(6, 1, 6, 1)
         quantise_h(7, 1, (0,))
         join(7, 1, 7, 1)
+        quantise_h(6, 1, (0, 1))
+        answer(6, 1, "s", 4)
         quantise_h(7, 1, (1,))
         answer(7, 1, "ssss", 1)
-        planes(0, 2)
-        planes(2, 2)
+        planes(0, 4)
         round_y(4, 2, "v")
         planes(4, 2)
         store_words(0, 6)
-        for v in range(2):
-            round_y(6 + v, 1, "v")
-            planes(6 + v, 1)
+        round_y(6, 1, "v")
+        planes(6, 1)
+        round_y(7, 1, "v")
+        planes(7, 1)
         store_words(6, 2)
         for q in range(4):
             queue = nc.sync if q % 2 == 0 else nc.scalar

@@ -21,7 +21,7 @@ PASS = 512
 HALF = 512
 CHUNKS = [(0, 512), (512, 512)]
 UNITS = [(c0, width, b) for c0, width in CHUNKS for b in range(2)]
-GAIN_ENG = ["gggg", "gggg", "gggg", "ssgg"]
+GAIN_ENG = ["gggg", "gggg", "gggg", "ssss"]
 BANKS = {"a": (0, 1, 2, 3, 4, 5, 6, 7), "b": (0, 1, 2, 3, 4, 5, 6, 7), "c": (0, 1, 2, 3), "y": (4, 5, 6, 7), "z": (7, 0, 1, 2)}
 A_FIRST = ()
 GAIN_BANK = 7
@@ -78,7 +78,9 @@ def tile_list_region_question_answer_kernel(
         w3_raw = shared.tile([P, H], I32, name="w3_raw", offset=16 * KB)
         w2_raw = shared.tile([P, H // 2], I32, name="w2_raw", offset=21 * KB)
         w_sraw = shared.tile([P, H], U8, name="w_sraw", offset=23 * KB)
-        w1_raw = [shared.tile([P, 4, PASS], F32, name=f"w1_raw{b}", offset=(24 + 8 * b) * KB) for b in range(2)]
+        w1_raw = [shared.tile([P, 4, PASS // 2], F32, name=f"w1_raw{i}", offset=(24 + 4 * i) * KB) for i in range(2)]
+        w1_rest = shared.tile([P, 4, PASS], F32, name="w1_rest", offset=32 * KB)
+        w1_parts = [w1_raw[0][:], w1_raw[1][:], w1_rest[:, :, 0 : PASS // 2], w1_rest[:, :, PASS // 2 : PASS]]
         w4_raw = [shared.tile([P, 4, N], F32, name=f"w4_raw{b}", offset=(40 + 8 * b) * KB) for b in range(2)]
         gain_rows = shared.tile([P, 2 * P], F32, name="gain_rows", offset=56 * KB)
         bias_col = shared.tile([P, 4], F32, name="bias_col", offset=57 * KB)
@@ -87,7 +89,11 @@ def tile_list_region_question_answer_kernel(
         nc.vector.memset(gain_rows[:], 0.0)
 
         def load_w1(b):
-            nc.sync.dma_start(out=w1_raw[b][:], in_=w1_rows[:, :, PASS * b : PASS * (b + 1)])
+            if b == 0:
+                for i in range(2):
+                    nc.sync.dma_start(out=w1_raw[i][:], in_=w1_rows[:, :, PASS // 2 * i : PASS // 2 * (i + 1)])
+            else:
+                nc.sync.dma_start(out=w1_rest[:], in_=w1_rows[:, :, PASS : 2 * PASS])
 
         def load_w4(b):
             rows = w4[PASS * b : PASS * (b + 1), :].rearrange("(q t e) n -> t q e n", t=4, e=4)
@@ -140,10 +146,9 @@ def tile_list_region_question_answer_kernel(
         def prepare_w1(b):
             grouped = keep.tile([P, 4 * PASS], BF16, name=f"w1_grouped{b}", align_bytes=64)
             dst = grouped[:].rearrange("p (t q e j) -> p q t j e", t=4, e=4, j=4)
-            src = w1_raw[b][:].rearrange("p j (q t e) -> p q t j e", t=4, e=4)
             for u in range(2):
-                part = slice(32 // 2 * u, 32 // 2 * (u + 1))
-                nc.scalar.copy(out=dst[:, part], in_=src[:, part])
+                src = w1_parts[2 * b + u].rearrange("p j (q t e) -> p q t j e", t=4, e=4)
+                nc.scalar.copy(out=dst[:, 16 * u : 16 * (u + 1)], in_=src)
             codes = keep.tile([P, PASS], U32, name=f"w1_codes{b}", align_bytes=64)
             scales = keep.tile([P, PASS], U8, name=f"w1_scales{b}", align_bytes=64)
             nc.vector.quantize_mx(out=codes[:].bitcast(FP8X4), scales=scales[:], in_=grouped[:])
@@ -340,31 +345,21 @@ def tile_list_region_question_answer_kernel(
                         )
             nc.sync.dma_start(out=out_rows[:, :, P * c : P * c + width], in_=y[c][:].rearrange("p (s j) -> p s j", s=4))
 
-        y_grouped = {}
+        y_rounded = keep.tile([P, 4 * S], BF16, name="y_rounded", align_bytes=64)
 
-        def round_y(c, chunks, cast):
-            y_grouped[c] = keep.tile([P, 4 * P * chunks], BF16, name=f"y_grouped{c}", align_bytes=64)
-            dst = y_grouped[c][:].rearrange("p (c i s) -> p c s i", i=4, s=4)
+        def round_y(c, chunks, eng):
+            dst = y_rounded[:, 4 * P * c : 4 * P * (c + chunks)].rearrange("p (c i s) -> p c s i", i=4, s=4)
             src = y[c][:].rearrange("p (s c i) -> p c s i", s=4, i=4)
-            size = 32 * chunks // len(cast)
-            for n, eng in enumerate(cast):
-                part = slice(size * n, size * (n + 1))
-                if eng == "s":
-                    nc.scalar.copy(out=dst[:, part], in_=src[:, part])
-                elif eng == "g":
-                    cols = slice(4 * size * n, 4 * size * (n + 1))
-                    nc.gpsimd.tensor_scalar(
-                        y_grouped[c][:].rearrange("p (j s) -> p j s", s=4)[:, cols],
-                        y[c][:].rearrange("p (s j) -> p j s", s=4)[:, cols], 1.0, 0.0, ALU.mult, ALU.add,
-                    )
-                else:
-                    nc.vector.tensor_copy(out=dst[:, part], in_=src[:, part])
+            if eng == "s":
+                nc.scalar.copy(out=dst, in_=src)
+            else:
+                nc.vector.tensor_copy(out=dst, in_=src)
 
         y_codes = keep.tile([P, S], U32, name="y_codes", align_bytes=64)
 
         def planes(c, chunks):
             cols = slice(P * c, P * (c + chunks))
-            nc.vector.quantize_mx(out=y_codes[:, cols].bitcast(FP8X4), scales=y_scales[:, cols], in_=y_grouped[c][:])
+            nc.vector.quantize_mx(out=y_codes[:, cols].bitcast(FP8X4), scales=y_scales[:, cols], in_=y_rounded[:, 4 * P * c : 4 * P * (c + chunks)])
 
         def store_words(c, chunks):
             cols = slice(P * c, P * (c + chunks))
@@ -387,40 +382,38 @@ def tile_list_region_question_answer_kernel(
         spread_gain()
         region(2)
         region(3)
-        gate(0)
-        gate(1)
-        cast_w4(0, 0, 1, "s")
-        gate(2)
-        cast_w4(1, 0, 1, "s")
-        gate(3)
-        join_piece(0, 4)
+        cast_w4(0, 0, 1, "v")
+        cast_w4(1, 0, 1, "v")
         quantise_w4()
-        quantise_h(0, 4, (0, 1))
-        answer(0, 4, "ssss", 1)
-        round_y(0, 4, "ss")
-        join(4, 0, 4, 2)
-        join(5, 0, 4, 2)
-        join(6, 0, 6, 1)
-        join(4, 1, 4, 2)
-        join(5, 1, 4, 2)
-        join(7, 0, 7, 1)
+        for u in range(4):
+            gate(u)
+        join_piece(0, 2)
+        quantise_h(0, 2, (0, 1))
+        answer(0, 2, "ss", 2)
+        round_y(0, 2, "s")
+        join_piece(2, 2)
+        quantise_h(2, 2, (0, 1))
+        answer(2, 2, "ss", 2)
+        round_y(2, 2, "s")
+        join_piece(4, 2)
         quantise_h(4, 2, (0, 1))
         answer(4, 2, "ss", 2)
-        join(6, 1, 6, 1)
-        quantise_h(7, 1, (0,))
-        join(7, 1, 7, 1)
+        join_piece(6, 1)
         quantise_h(6, 1, (0, 1))
         answer(6, 1, "s", 4)
+        join(7, 0, 7, 1)
+        quantise_h(7, 1, (0,))
+        join(7, 1, 7, 1)
         quantise_h(7, 1, (1,))
         answer(7, 1, "ssss", 1)
         planes(0, 4)
+        store_words(0, 4)
         round_y(4, 2, "v")
         planes(4, 2)
-        store_words(0, 6)
-        round_y(6, 1, "v")
-        planes(6, 1)
-        round_y(7, 1, "v")
-        planes(7, 1)
+        store_words(4, 2)
+        for v in range(2):
+            round_y(6 + v, 1, "v")
+            planes(6 + v, 1)
         store_words(6, 2)
         for q in range(4):
             queue = nc.sync if q % 2 == 0 else nc.scalar

@@ -26,7 +26,7 @@ BANKS = {"a": (0, 1, 2, 3, 4, 5, 6, 7), "b": (0, 1, 2, 3, 4, 5, 6, 7), "c": (0, 
 A_FIRST = ()
 GAIN_BANK = 7
 KB = 1024
-STAGING = 58 * KB
+STAGING = 66 * KB
 TANH_SPAN = (2, 2, 2, 2)
 RUN = 2
 
@@ -77,23 +77,19 @@ def tile_list_region_question_answer_kernel(
         tab_w = shared.tile([P, T], U32, name="tab_w", offset=0, align_bytes=64)
         w3_raw = shared.tile([P, H], I32, name="w3_raw", offset=16 * KB)
         w2_raw = shared.tile([P, H // 2], I32, name="w2_raw", offset=21 * KB)
-        w_sraw = shared.tile([P, H], U8, name="w_sraw", offset=23 * KB)
-        w1_raw = [shared.tile([P, 4, PASS // 2], F32, name=f"w1_raw{i}", offset=(24 + 4 * i) * KB) for i in range(2)]
-        w1_rest = shared.tile([P, 4, PASS], F32, name="w1_rest", offset=32 * KB)
-        w1_parts = [w1_raw[0][:], w1_raw[1][:], w1_rest[:, :, 0 : PASS // 2], w1_rest[:, :, PASS // 2 : PASS]]
-        w4_raw = [shared.tile([P, 4, N], F32, name=f"w4_raw{b}", offset=(40 + 8 * b) * KB) for b in range(2)]
-        gain_rows = shared.tile([P, 2 * P], F32, name="gain_rows", offset=56 * KB)
-        bias_col = shared.tile([P, 4], F32, name="bias_col", offset=57 * KB)
+        w_sraw = shared.tile([P, H], U8, name="w_sraw", offset=20 * KB)
+        w1_raw = [shared.tile([P, 4, PASS // 2], F32, name=f"w1_raw{i}", offset=(24 + 4 * i) * KB) for i in range(4)]
+        w1_parts = [raw[:] for raw in w1_raw]
+        w4_raw = [shared.tile([P, 4, N], F32, name=f"w4_raw{b}", offset=(48 + 8 * b) * KB) for b in range(2)]
+        gain_rows = shared.tile([P, 2 * P], F32, name="gain_rows", offset=64 * KB)
+        bias_col = shared.tile([P, 4], F32, name="bias_col", offset=65 * KB)
         w1_rows = w1.rearrange("(p j) c -> p j c", j=4)
         nc.vector.memset(w_sraw[:].bitcast(I32), 0)
         nc.vector.memset(gain_rows[:], 0.0)
 
         def load_w1(b):
-            if b == 0:
-                for i in range(2):
-                    nc.sync.dma_start(out=w1_raw[i][:], in_=w1_rows[:, :, PASS // 2 * i : PASS // 2 * (i + 1)])
-            else:
-                nc.sync.dma_start(out=w1_rest[:], in_=w1_rows[:, :, PASS : 2 * PASS])
+            for i in range(2 * b, 2 * b + 2):
+                nc.sync.dma_start(out=w1_raw[i][:], in_=w1_rows[:, :, PASS // 2 * i : PASS // 2 * (i + 1)])
 
         def load_w4(b):
             rows = w4[PASS * b : PASS * (b + 1), :].rearrange("(q t e) n -> t q e n", t=4, e=4)
@@ -119,8 +115,8 @@ def tile_list_region_question_answer_kernel(
             nc.sync.dma_start(out=bias_col[:], in_=bias.rearrange("(p s) -> p s", s=4))
 
         load_w1(0)
-        load_w1(1)
         load_table()
+        load_w1(1)
         load_w2()
         load_w3()
         load_scales(w_sraw, w2_scales)
@@ -144,7 +140,7 @@ def tile_list_region_question_answer_kernel(
         w1_q = [None, None]
 
         def prepare_w1(b):
-            grouped = keep.tile([P, 4 * PASS], BF16, name=f"w1_grouped{b}", align_bytes=64)
+            grouped = shared.tile([P, 4 * PASS], BF16, name=f"w1_grouped{b}", offset=(74 - 5 * b) * KB, align_bytes=64)
             dst = grouped[:].rearrange("p (t q e j) -> p q t j e", t=4, e=4, j=4)
             for u in range(2):
                 src = w1_parts[2 * b + u].rearrange("p j (q t e) -> p q t j e", t=4, e=4)
@@ -156,13 +152,16 @@ def tile_list_region_question_answer_kernel(
 
         got_w = [[None] * 2 for i in range(3)]
 
-        def gather_words(i, half):
-            g = keep.tile([P, HALF], U32, name=f"got_w{i}{half}", align_bytes=64)
+        def gather_words(i, half, offset=None):
+            if offset is None:
+                g = keep.tile([P, HALF], U32, name=f"got_w{i}{half}", align_bytes=64)
+            else:
+                g = shared.tile([P, HALF], U32, name=f"got_w{i}{half}", offset=offset, align_bytes=64)
             nc.vector.tensor_copy(g[:], tab_w[:].indirect(lists[i][:, 32 * half : 32 * (half + 1)]))
             got_w[i][half] = g[:]
 
-        def gather_list(i):
-            g = keep.tile([P, S], U32, name=f"got_w{i}", align_bytes=64)
+        def gather_list(i, offset):
+            g = shared.tile([P, S], U32, name=f"got_w{i}", offset=offset, align_bytes=64)
             nc.vector.tensor_copy(g[:], tab_w[:].indirect(lists[i][:]))
             for half in range(2):
                 got_w[i][half] = g[:, HALF * half : HALF * (half + 1)]
@@ -191,11 +190,8 @@ def tile_list_region_question_answer_kernel(
         w4_grouped = {}
 
         def cast_w4(b, u, parts, eng):
-            if not w4_grouped:
-                both = shared.tile([P, 2 * 4 * N], BF16, name="w4_grouped", offset=32 * KB, align_bytes=64)
-                w4_grouped["both"] = both[:]
-                for i in range(2):
-                    w4_grouped[i] = both[:, 4 * N * i : 4 * N * (i + 1)]
+            if b not in w4_grouped:
+                w4_grouped[b] = shared.tile([P, 4 * N], BF16, name=f"w4_grouped{b}", offset=32 * KB * b, align_bytes=64)[:]
             dst = w4_grouped[b].rearrange("p (s m t) -> p m t s", s=4, t=4)
             src = w4_raw[b][:].rearrange("p t (m s) -> p m t s", s=4)
             share = slice(4 // parts * u, 4 // parts * (u + 1))
@@ -203,18 +199,17 @@ def tile_list_region_question_answer_kernel(
                 nc.scalar.copy(out=dst[:, :, :, share], in_=src[:, :, :, share])
             elif eng == "g":
                 nc.gpsimd.tensor_scalar(
-                    w4_grouped[b].rearrange("p (s m t) -> p s m t", s=4, t=4)[:, share],
-                    w4_raw[b][:].rearrange("p t (m s) -> p s m t", s=4)[:, share], 1.0, 0.0, ALU.mult, ALU.add,
+                    w4_grouped[b].rearrange("p (s m t) -> p m s t", s=4, t=4)[:, P // parts * u : P // parts * (u + 1)],
+                    w4_raw[b][:].rearrange("p t (m s) -> p m s t", s=4)[:, P // parts * u : P // parts * (u + 1)], 1.0, 0.0, ALU.mult, ALU.add,
                 )
             else:
                 nc.vector.tensor_copy(out=dst[:, :, :, share], in_=src[:, :, :, share])
 
-        def quantise_w4():
-            codes = keep.tile([P, 2 * N], U32, name="w4_codes", align_bytes=64)
-            scales = keep.tile([P, 2 * N], U8, name="w4_scales", align_bytes=64)
-            nc.vector.quantize_mx(out=codes[:].bitcast(FP8X4), scales=scales[:], in_=w4_grouped["both"])
-            for b in range(2):
-                w4_q[b] = (codes[:, N * b : N * (b + 1)], scales[:, N * b : N * (b + 1)])
+        def quantise_w4(b):
+            codes = shared.tile([P, N], U32, name=f"w4_codes{b}", offset=(36 - 6 * b) * KB, align_bytes=64)
+            scales = keep.tile([P, N], U8, name=f"w4_scales{b}", align_bytes=64)
+            nc.vector.quantize_mx(out=codes[:].bitcast(FP8X4), scales=scales[:], in_=w4_grouped[b])
+            w4_q[b] = (codes[:], scales[:])
 
         def moving(i, j0, width):
             half, c0 = divmod(j0, HALF)
@@ -243,7 +238,9 @@ def tile_list_region_question_answer_kernel(
                         out=a_ps[:, width * i : width * (i + 1)], lhsT=codes[:, cols].bitcast(FP8X4),
                         lhsT_scale=scales[:, cols], rhs=rhs, rhs_scale=rhs_s, start=True, stop=True,
                     )
-                if n == 0:
+                if n == 0 and b == 0:
+                    a_sb[u] = shared.tile([P, 4 * width], F32, name=f"a_sb{u}", offset=(30 + 4 * u) * KB)
+                elif n == 0:
                     a_sb[u] = keep.tile([P, 4 * width], F32, name=f"a_sb{u}")
                 nc.scalar.copy(out=a_sb[u][:, HALF * n : HALF * (n + 1)], in_=a_ps[:])
 
@@ -343,13 +340,16 @@ def tile_list_region_question_answer_kernel(
                             out=y[c][:, width * s : width * (s + 1)], in_=y_ps[:, ss, :], func=ACT.Identity,
                             bias=bias_col[:, s : s + 1],
                         )
-            nc.sync.dma_start(out=out_rows[:, :, P * c : P * c + width], in_=y[c][:].rearrange("p (s j) -> p s j", s=4))
+                if width == HALF:
+                    nc.sync.dma_start(out=out_rows[:, u, P * c : P * c + width], in_=y[c][:, width * u : width * (u + 1)])
+            if width < HALF:
+                nc.sync.dma_start(out=out_rows[:, :, P * c : P * c + width], in_=y[c][:].rearrange("p (s j) -> p s j", s=4))
 
         y_rounded = keep.tile([P, 4 * S], BF16, name="y_rounded", align_bytes=64)
 
-        def round_y(c, chunks, eng):
+        def round_y(first, c, chunks, eng):
             dst = y_rounded[:, 4 * P * c : 4 * P * (c + chunks)].rearrange("p (c i s) -> p c s i", i=4, s=4)
-            src = y[c][:].rearrange("p (s c i) -> p c s i", s=4, i=4)
+            src = y[first][:].rearrange("p (s c i) -> p c s i", s=4, i=4)[:, P // 4 * (c - first) : P // 4 * (c - first + chunks)]
             if eng == "s":
                 nc.scalar.copy(out=dst, in_=src)
             else:
@@ -370,49 +370,63 @@ def tile_list_region_question_answer_kernel(
         gather_scales(2)
         prepare_w1(0)
         prepare_w1(1)
-        gather_words(0, 0)
-        gather_words(0, 1)
-        gather_list(1)
-        gather_list(2)
-        dealt["w2_w"] = deal("w2_w", w2_raw[:], 2, 0)
-        dealt["w_s"] = deal("w_s", w_sraw[:].bitcast(I32), 1)
-        dealt["w3_w"] = deal("w3_w", w3_raw[:], 4, 23 * KB)
+        gather_words(0, 0, 74 * KB)
+        gather_words(0, 1, 76 * KB)
+        gather_words(1, 0)
+        gather_words(1, 1)
+        dealt["w2_w"] = deal("w2_w", w2_raw[:], 2, 71 * KB)
+        dealt["w3_w"] = deal("w3_w", w3_raw[:], 4, 66 * KB)
+        dealt["w_s"] = deal("w_s", w_sraw[:].bitcast(I32), 1, 70 * KB)
+        gather_list(2, 19 * KB)
         region(0)
-        region(1)
-        spread_gain()
         region(2)
+        spread_gain()
+        region(1)
         region(3)
-        cast_w4(0, 0, 1, "v")
-        cast_w4(1, 0, 1, "v")
-        quantise_w4()
-        for u in range(4):
-            gate(u)
-        join_piece(0, 2)
+        cast_w4(0, 0, 1, "g")
+        gate(0)
+        gate(1)
+        cast_w4(1, 0, 1, "s")
+        gate(2)
+        gate(3)
+        join(0, 0, 0, 2)
+        join(1, 0, 0, 2)
+        join(0, 1, 0, 2)
+        join(1, 1, 0, 2)
+        join(2, 0, 2, 2)
+        join(3, 0, 2, 2)
+        quantise_w4(0)
+        quantise_w4(1)
         quantise_h(0, 2, (0, 1))
-        answer(0, 2, "ss", 2)
-        round_y(0, 2, "s")
-        join_piece(2, 2)
+        join(2, 1, 2, 2)
+        join(3, 1, 2, 2)
+        join(4, 0, 4, 2)
         quantise_h(2, 2, (0, 1))
-        answer(2, 2, "ss", 2)
-        round_y(2, 2, "s")
-        join_piece(4, 2)
+        join(5, 0, 4, 2)
+        join(4, 1, 4, 2)
+        join(5, 1, 4, 2)
+        join(6, 0, 6, 1)
         quantise_h(4, 2, (0, 1))
-        answer(4, 2, "ss", 2)
-        join_piece(6, 1)
-        quantise_h(6, 1, (0, 1))
-        answer(6, 1, "s", 4)
+        join(6, 1, 6, 1)
         join(7, 0, 7, 1)
-        quantise_h(7, 1, (0,))
+        quantise_h(6, 1, (0, 1))
         join(7, 1, 7, 1)
+        quantise_h(7, 1, (0,))
         quantise_h(7, 1, (1,))
+        answer(0, 2, "ss", 2)
+        answer(2, 2, "ss", 2)
+        round_y(0, 0, 2, "s")
+        answer(4, 2, "ss", 2)
+        round_y(2, 2, 2, "v")
+        answer(6, 1, "s", 4)
         answer(7, 1, "ssss", 1)
         planes(0, 4)
         store_words(0, 4)
-        round_y(4, 2, "v")
+        round_y(4, 4, 2, "v")
         planes(4, 2)
         store_words(4, 2)
         for v in range(2):
-            round_y(6 + v, 1, "v")
+            round_y(6 + v, 6 + v, 1, "v")
             planes(6 + v, 1)
         store_words(6, 2)
         for q in range(4):

@@ -21,7 +21,7 @@ PASS = 512
 HALF = 512
 CHUNKS = [(0, 512), (512, 512)]
 UNITS = [(c0, width, b) for c0, width in CHUNKS for b in range(2)]
-GAIN_ENG = ["gggg", "gggg", "gggg", "ssss"]
+GAIN_ENG = ["gggg", "ssss", "gggg", "ssss"]
 BANKS = {"a": (0, 1, 2, 3, 4, 5, 6, 7), "b": (0, 1, 2, 3, 4, 5, 6, 7), "c": (0, 1, 2, 3), "y": (4, 5, 6, 7), "z": (7, 0, 1, 2)}
 A_FIRST = ()
 GAIN_BANK = 7
@@ -55,10 +55,8 @@ def tile_list_region_question_answer_kernel(
 
 
         def load_scales(plane, rows, first=0):
-            for q in range(4):
-                nc.sync.dma_start(
-                    out=plane[32 * q + first : 32 * q + first + 4, :].bitcast(I32), in_=rows[0, 4 * q : 4 * q + 4, :].bitcast(I32)
-                )
+            for r in range(4):
+                nc.sync.dma_start(out=plane[first + r : P : 32, :].bitcast(I32), in_=rows[0, r:16:4, :].bitcast(I32))
 
         lists = []
         for i, src in enumerate((offs, offs2, offs3)):
@@ -75,9 +73,9 @@ def tile_list_region_question_answer_kernel(
             out=ident[:], in_=zeros[:, 0:P], compare_op=ALU.not_equal, fill=1.0, base=0, pattern=[[-1, P]], channel_multiplier=1
         )
         tab_w = shared.tile([P, T], U32, name="tab_w", offset=0, align_bytes=64)
-        w3_raw = shared.tile([P, H], I32, name="w3_raw", offset=16 * KB)
-        w2_raw = shared.tile([P, H // 2], I32, name="w2_raw", offset=21 * KB)
-        w_sraw = shared.tile([P, H], U8, name="w_sraw", offset=20 * KB)
+        w3_raw = shared.tile([P, H], I32, name="w3_raw", offset=20 * KB)
+        w2_raw = shared.tile([P, H // 2], I32, name="w2_raw", offset=17 * KB)
+        w_sraw = shared.tile([P, H], U8, name="w_sraw", offset=16 * KB)
         w1_raw = [shared.tile([P, 4, PASS // 2], F32, name=f"w1_raw{i}", offset=(24 + 4 * i) * KB) for i in range(4)]
         w1_parts = [raw[:] for raw in w1_raw]
         w4_raw = [shared.tile([P, 4, N], F32, name=f"w4_raw{b}", offset=(48 + 8 * b) * KB) for b in range(2)]
@@ -140,11 +138,16 @@ def tile_list_region_question_answer_kernel(
         w1_q = [None, None]
 
         def prepare_w1(b):
-            grouped = shared.tile([P, 4 * PASS], BF16, name=f"w1_grouped{b}", offset=(74 - 5 * b) * KB, align_bytes=64)
-            dst = grouped[:].rearrange("p (t q e j) -> p q t j e", t=4, e=4, j=4)
+            grouped = shared.tile([P, 4 * PASS], BF16, name=f"w1_grouped{b}", offset=(76 - 7 * b) * KB, align_bytes=64)
             for u in range(2):
-                src = w1_parts[2 * b + u].rearrange("p j (q t e) -> p q t j e", t=4, e=4)
-                nc.scalar.copy(out=dst[:, 16 * u : 16 * (u + 1)], in_=src)
+                if b == 0:
+                    dst = grouped[:].rearrange("p (t q e j) -> p q t j e", t=4, e=4, j=4)
+                    src = w1_parts[2 * b + u].rearrange("p j (q t e) -> p q t j e", t=4, e=4)
+                    nc.scalar.copy(out=dst[:, 16 * u : 16 * (u + 1)], in_=src)
+                else:
+                    dst = grouped[:].rearrange("p (t q e j) -> p q t e j", t=4, e=4, j=4)
+                    src = w1_parts[2 * b + u].rearrange("p j (q t e) -> p q t e j", t=4, e=4)
+                    nc.gpsimd.tensor_scalar(dst[:, 16 * u : 16 * (u + 1)], src, 1.0, 0.0, ALU.mult, ALU.add)
             codes = keep.tile([P, PASS], U32, name=f"w1_codes{b}", align_bytes=64)
             scales = keep.tile([P, PASS], U8, name=f"w1_scales{b}", align_bytes=64)
             nc.vector.quantize_mx(out=codes[:].bitcast(FP8X4), scales=scales[:], in_=grouped[:])
@@ -190,8 +193,11 @@ def tile_list_region_question_answer_kernel(
         w4_grouped = {}
 
         def cast_w4(b, u, parts, eng):
-            if b not in w4_grouped:
-                w4_grouped[b] = shared.tile([P, 4 * N], BF16, name=f"w4_grouped{b}", offset=32 * KB * b, align_bytes=64)[:]
+            if not w4_grouped:
+                both = shared.tile([P, 2 * 4 * N], BF16, name="w4_grouped", offset=22 * KB, align_bytes=64)
+                w4_grouped["both"] = both[:]
+                for i in range(2):
+                    w4_grouped[i] = both[:, 4 * N * i : 4 * N * (i + 1)]
             dst = w4_grouped[b].rearrange("p (s m t) -> p m t s", s=4, t=4)
             src = w4_raw[b][:].rearrange("p t (m s) -> p m t s", s=4)
             share = slice(4 // parts * u, 4 // parts * (u + 1))
@@ -205,11 +211,12 @@ def tile_list_region_question_answer_kernel(
             else:
                 nc.vector.tensor_copy(out=dst[:, :, :, share], in_=src[:, :, :, share])
 
-        def quantise_w4(b):
-            codes = shared.tile([P, N], U32, name=f"w4_codes{b}", offset=(36 - 6 * b) * KB, align_bytes=64)
-            scales = keep.tile([P, N], U8, name=f"w4_scales{b}", align_bytes=64)
-            nc.vector.quantize_mx(out=codes[:].bitcast(FP8X4), scales=scales[:], in_=w4_grouped[b])
-            w4_q[b] = (codes[:], scales[:])
+        def quantise_w4():
+            codes = shared.tile([P, 2 * N], U32, name="w4_codes", offset=41 * KB, align_bytes=64)
+            scales = shared.tile([P, 2 * N], U8, name="w4_scales", offset=40 * KB, align_bytes=64)
+            nc.vector.quantize_mx(out=codes[:].bitcast(FP8X4), scales=scales[:], in_=w4_grouped["both"])
+            for b in range(2):
+                w4_q[b] = (codes[:, N * b : N * (b + 1)], scales[:, N * b : N * (b + 1)])
 
         def moving(i, j0, width):
             half, c0 = divmod(j0, HALF)
@@ -238,8 +245,8 @@ def tile_list_region_question_answer_kernel(
                         out=a_ps[:, width * i : width * (i + 1)], lhsT=codes[:, cols].bitcast(FP8X4),
                         lhsT_scale=scales[:, cols], rhs=rhs, rhs_scale=rhs_s, start=True, stop=True,
                     )
-                if n == 0 and b == 0:
-                    a_sb[u] = shared.tile([P, 4 * width], F32, name=f"a_sb{u}", offset=(30 + 4 * u) * KB)
+                if n == 0 and u == 0:
+                    a_sb[u] = shared.tile([P, 4 * width], F32, name=f"a_sb{u}", offset=40 * KB)
                 elif n == 0:
                     a_sb[u] = keep.tile([P, 4 * width], F32, name=f"a_sb{u}")
                 nc.scalar.copy(out=a_sb[u][:, HALF * n : HALF * (n + 1)], in_=a_ps[:])
@@ -247,7 +254,10 @@ def tile_list_region_question_answer_kernel(
         def gate(u):
             c0, width, b = UNITS[u]
             rhs, rhs_s = moving(1, c0, width)
-            gated[u] = keep.tile([P, 4 * width], F32, name=f"gated{u}")
+            if u == 0:
+                gated[u] = shared.tile([P, 4 * width], F32, name=f"gated{u}", offset=56 * KB)
+            else:
+                gated[u] = keep.tile([P, 4 * width], F32, name=f"gated{u}")
             for n, slices in enumerate(steps(u)):
                 b_ps = bank("b", [P, HALF])
                 for i, t in enumerate(slices):
@@ -340,9 +350,12 @@ def tile_list_region_question_answer_kernel(
                             out=y[c][:, width * s : width * (s + 1)], in_=y_ps[:, ss, :], func=ACT.Identity,
                             bias=bias_col[:, s : s + 1],
                         )
-                if width == HALF:
-                    nc.sync.dma_start(out=out_rows[:, u, P * c : P * c + width], in_=y[c][:, width * u : width * (u + 1)])
-            if width < HALF:
+                if c == 4:
+                    nc.sync.dma_start(
+                        out=out_rows[:, 2 * u : 2 * u + 2, P * c : P * c + width],
+                        in_=y[c][:, 2 * width * u : 2 * width * (u + 1)].rearrange("p (s j) -> p s j", s=2),
+                    )
+            if c != 4:
                 nc.sync.dma_start(out=out_rows[:, :, P * c : P * c + width], in_=y[c][:].rearrange("p (s j) -> p s j", s=4))
 
         y_rounded = keep.tile([P, 4 * S], BF16, name="y_rounded", align_bytes=64)
@@ -370,34 +383,30 @@ def tile_list_region_question_answer_kernel(
         gather_scales(2)
         prepare_w1(0)
         prepare_w1(1)
-        gather_words(0, 0, 74 * KB)
-        gather_words(0, 1, 76 * KB)
-        gather_words(1, 0)
-        gather_words(1, 1)
-        dealt["w2_w"] = deal("w2_w", w2_raw[:], 2, 71 * KB)
-        dealt["w3_w"] = deal("w3_w", w3_raw[:], 4, 66 * KB)
-        dealt["w_s"] = deal("w_s", w_sraw[:].bitcast(I32), 1, 70 * KB)
-        gather_list(2, 19 * KB)
+        gather_words(0, 0, 75 * KB)
+        gather_words(0, 1, 77 * KB)
+        gather_list(1, 79 * KB)
+        dealt["w_s"] = deal("w_s", w_sraw[:].bitcast(I32), 1, 37 * KB)
+        dealt["w2_w"] = deal("w2_w", w2_raw[:], 2, 38 * KB)
+        dealt["w3_w"] = deal("w3_w", w3_raw[:], 4, 33 * KB)
+        gather_list(2, 16 * KB)
         region(0)
         region(2)
         spread_gain()
         region(1)
         region(3)
         cast_w4(0, 0, 1, "g")
-        gate(0)
-        gate(1)
-        cast_w4(1, 0, 1, "s")
-        gate(2)
-        gate(3)
+        cast_w4(1, 0, 1, "g")
+        for u in range(4):
+            gate(u)
+        quantise_w4()
         join(0, 0, 0, 2)
         join(1, 0, 0, 2)
         join(0, 1, 0, 2)
         join(1, 1, 0, 2)
         join(2, 0, 2, 2)
-        join(3, 0, 2, 2)
-        quantise_w4(0)
-        quantise_w4(1)
         quantise_h(0, 2, (0, 1))
+        join(3, 0, 2, 2)
         join(2, 1, 2, 2)
         join(3, 1, 2, 2)
         join(4, 0, 4, 2)
@@ -405,6 +414,10 @@ def tile_list_region_question_answer_kernel(
         join(5, 0, 4, 2)
         join(4, 1, 4, 2)
         join(5, 1, 4, 2)
+        answer(0, 2, "ss", 2)
+        round_y(0, 0, 2, "s")
+        planes(0, 2)
+        store_words(0, 2)
         join(6, 0, 6, 1)
         quantise_h(4, 2, (0, 1))
         join(6, 1, 6, 1)
@@ -413,24 +426,23 @@ def tile_list_region_question_answer_kernel(
         join(7, 1, 7, 1)
         quantise_h(7, 1, (0,))
         quantise_h(7, 1, (1,))
-        answer(0, 2, "ss", 2)
         answer(2, 2, "ss", 2)
-        round_y(0, 0, 2, "s")
+        round_y(2, 2, 2, "s")
         answer(4, 2, "ss", 2)
-        round_y(2, 2, 2, "v")
         answer(6, 1, "s", 4)
         answer(7, 1, "ssss", 1)
-        planes(0, 4)
-        store_words(0, 4)
+        planes(2, 2)
+        store_words(2, 2)
         round_y(4, 4, 2, "v")
+        round_y(6, 6, 1, "v")
         planes(4, 2)
         store_words(4, 2)
-        for v in range(2):
-            round_y(6 + v, 6 + v, 1, "v")
-            planes(6 + v, 1)
+        round_y(7, 7, 1, "v")
+        planes(6, 1)
+        planes(7, 1)
         store_words(6, 2)
         for q in range(4):
             queue = nc.sync if q % 2 == 0 else nc.scalar
             queue.dma_start(
-                out=out_2[0, 4 * q : 4 * q + 4, :].bitcast(I32), in_=y_scales[32 * q : 32 * q + 4, :].bitcast(I32)
+                out=out_2[0, q:16:4, :].bitcast(I32), in_=y_scales[q:P:32, :].bitcast(I32)
             )

@@ -24,7 +24,7 @@ UNITS = [(c0, width, b) for c0, width in CHUNKS for b in range(2)]
 GAIN_ENG = ["gggg", "ssss", "gggg", "ssss"]
 BANKS = {"a": (0, 1, 2, 3, 4, 5, 6, 7), "b": (0, 1, 2, 3, 4, 5, 6, 7), "c": (0, 1, 2, 3), "y": (4, 5, 6, 7), "z": (7, 0, 1, 2)}
 A_FIRST = ()
-GAIN_BANK = 7
+GAIN_BANK = 0
 KB = 1024
 STAGING = 66 * KB
 TANH_SPAN = (2, 2, 2, 2)
@@ -85,9 +85,8 @@ def tile_list_region_question_answer_kernel(
         nc.vector.memset(w_sraw[:].bitcast(I32), 0)
         nc.vector.memset(gain_rows[:], 0.0)
 
-        def load_w1(b):
-            for i in range(2 * b, 2 * b + 2):
-                nc.sync.dma_start(out=w1_raw[i][:], in_=w1_rows[:, :, PASS // 2 * i : PASS // 2 * (i + 1)])
+        def load_w1(i):
+            nc.sync.dma_start(out=w1_raw[i][:], in_=w1_rows[:, :, PASS // 2 * i : PASS // 2 * (i + 1)])
 
         def load_w4(b):
             rows = w4[PASS * b : PASS * (b + 1), :].rearrange("(q t e) n -> t q e n", t=4, e=4)
@@ -113,12 +112,14 @@ def tile_list_region_question_answer_kernel(
             nc.sync.dma_start(out=bias_col[:], in_=bias.rearrange("(p s) -> p s", s=4))
 
         load_w1(0)
-        load_table()
         load_w1(1)
+        load_table()
+        load_w1(2)
+        load_scales(w_sraw, w2_scales)
+        load_w1(3)
+        load_scales(w_sraw, w3_scales, 4)
         load_w2()
         load_w3()
-        load_scales(w_sraw, w2_scales)
-        load_scales(w_sraw, w3_scales, 4)
         load_gain()
         load_w4(0)
         load_w4(1)
@@ -254,8 +255,8 @@ def tile_list_region_question_answer_kernel(
         def gate(u):
             c0, width, b = UNITS[u]
             rhs, rhs_s = moving(1, c0, width)
-            if u == 0:
-                gated[u] = shared.tile([P, 4 * width], F32, name=f"gated{u}", offset=56 * KB)
+            if u % 2 == 0:
+                gated[u] = shared.tile([P, 4 * width], F32, name=f"gated{u}", offset=(56 - 17 * u) * KB)
             else:
                 gated[u] = keep.tile([P, 4 * width], F32, name=f"gated{u}")
             for n, slices in enumerate(steps(u)):
@@ -268,6 +269,8 @@ def tile_list_region_question_answer_kernel(
                     )
                 ab = a_sb[u][:, HALF * n : HALF * (n + 1)]
                 nc.vector.tensor_tensor(ab, ab, b_ps[:], ALU.mult)
+                if u == 0 and n == 0:
+                    spread_gain()
                 span = TANH_SPAN[u]
                 if (n + 1) % span == 0:
                     th = a_sb[u][:, HALF * (n + 1 - span) : HALF * (n + 1)]
@@ -365,6 +368,12 @@ def tile_list_region_question_answer_kernel(
             src = y[first][:].rearrange("p (s c i) -> p c s i", s=4, i=4)[:, P // 4 * (c - first) : P // 4 * (c - first + chunks)]
             if eng == "s":
                 nc.scalar.copy(out=dst, in_=src)
+            elif eng == "g":
+                nc.gpsimd.tensor_scalar(
+                    y_rounded[:, 4 * P * c : 4 * P * (c + chunks)].rearrange("p (j s) -> p j s", s=4),
+                    y[first][:].rearrange("p (s j) -> p j s", s=4)[:, P * (c - first) : P * (c - first + chunks)],
+                    1.0, 0.0, ALU.mult, ALU.add,
+                )
             else:
                 nc.vector.tensor_copy(out=dst, in_=src)
 
@@ -383,7 +392,7 @@ def tile_list_region_question_answer_kernel(
         gather_scales(2)
         prepare_w1(0)
         prepare_w1(1)
-        gather_words(0, 0, 75 * KB)
+        gather_words(0, 0)
         gather_words(0, 1, 77 * KB)
         gather_list(1, 79 * KB)
         dealt["w_s"] = deal("w_s", w_sraw[:].bitcast(I32), 1, 37 * KB)
@@ -392,7 +401,6 @@ def tile_list_region_question_answer_kernel(
         gather_list(2, 16 * KB)
         region(0)
         region(2)
-        spread_gain()
         region(1)
         region(3)
         cast_w4(0, 0, 1, "g")
@@ -415,7 +423,7 @@ def tile_list_region_question_answer_kernel(
         join(4, 1, 4, 2)
         join(5, 1, 4, 2)
         answer(0, 2, "ss", 2)
-        round_y(0, 0, 2, "s")
+        round_y(0, 0, 2, "g")
         planes(0, 2)
         store_words(0, 2)
         join(6, 0, 6, 1)

from contextlib import ExitStack

import concourse.mybir as mybir

K, T, S, H, N = 512, 4096, 1024, 1024, 512
FLOPS = 2 * (3 * K * H * S + H * N * S)

F32 = mybir.dt.float32
BF16 = mybir.dt.bfloat16
I32 = mybir.dt.int32
U32 = mybir.dt.uint32
U16 = mybir.dt.uint16
U8 = mybir.dt.uint8
FP8X4 = mybir.dt.float8_e4m3fn_x4
FP4X4 = mybir.dt.float4_e2m1fn_x4
ACT = mybir.ActivationFunctionType
ALU = mybir.AluOpType

P = 128
PASS = 512
HALF = 512
CHUNKS = [(0, 512), (512, 512)]
UNITS = [(c0, width, b) for c0, width in CHUNKS for b in range(2)]
GAIN_ENG = ["gggg", "ssss", "gggg", "ssss"]
BANKS = {"a": (0, 1, 2, 3, 4, 5, 6, 7), "b": (0, 1, 2, 3, 4, 5, 6, 7), "c": (0, 1, 2, 3), "y": (4, 5, 6, 7), "z": (7, 0, 1, 2)}
A_FIRST = ()
GAIN_BANK = 0
KB = 1024
STAGING = 66 * KB
TANH_SPAN = (2, 2, 2, 2)
RUN = 2


def tile_list_region_question_answer_kernel(
    tc, tab_words, tab_scales, offs, offs2, offs3, w1, w2_words, w2_scales, w3_words, w3_scales, w4, gain, bias,
    out_0, out_1, out_2,
):
    nc = tc.nc
    with ExitStack() as ctx:
        keep = ctx.enter_context(tc.tile_pool(name="keep", bufs=1))
        shared = ctx.enter_context(tc.tile_pool(name="shared", bufs=1))
        psum = ctx.enter_context(tc.psum_pool(name="psum", bufs=1))
        used = {"a": [], "b": [], "c": [], "y": [], "g": [], "z": []}

        def bank(kind, shape):
            n = len(used[kind])
            used[kind].append(n)
            if kind == "a" and n < len(A_FIRST):
                place = A_FIRST[n]
            elif kind == "g":
                place = GAIN_BANK
            else:
                place = BANKS[kind][n % len(BANKS[kind])]
            return psum.tile(shape, F32, name=f"{kind}_bank{n}", offset=2048 * place)


        def load_scales(plane, rows, first=0):
            for r in range(4):
                nc.sync.dma_start(out=plane[first + r : P : 32, :].bitcast(I32), in_=rows[0, r:16:4, :].bitcast(I32))

        lists = []
        for i, src in enumerate((offs, offs2, offs3)):
            lst = keep.tile([P, S // 16], U16, name=f"list{i}")
            nc.sync.dma_start(lst[:], src)
            lists.append(lst)
        tab_s = keep.tile([P, T], U8, name="tab_s", align_bytes=64)
        nc.vector.memset(tab_s[:].bitcast(I32), 0)
        load_scales(tab_s, tab_scales)
        ident = keep.tile([P, P], F32, name="ident")
        zeros = shared.tile([P, STAGING // 4], F32, name="zeros", offset=0)
        nc.vector.memset(zeros[:, 0:P], 0.0)
        nc.gpsimd.affine_select(
            out=ident[:], in_=zeros[:, 0:P], compare_op=ALU.not_equal, fill=1.0, base=0, pattern=[[-1, P]], channel_multiplier=1
        )
        tab_w = shared.tile([P, T], U32, name="tab_w", offset=0, align_bytes=64)
        w3_raw = shared.tile([P, H], I32, name="w3_raw", offset=20 * KB)
        w2_raw = shared.tile([P, H // 2], I32, name="w2_raw", offset=17 * KB)
        w_sraw = shared.tile([P, H], U8, name="w_sraw", offset=16 * KB)
        w1_raw = [shared.tile([P, 4, PASS // 2], F32, name=f"w1_raw{i}", offset=(24 + 4 * i) * KB) for i in range(4)]
        w1_parts = [raw[:] for raw in w1_raw]
        w4_raw = [shared.tile([P, 4, N], F32, name=f"w4_raw{b}", offset=(48 + 8 * b) * KB) for b in range(2)]
        gain_rows = shared.tile([P, 2 * P], F32, name="gain_rows", offset=64 * KB)
        bias_col = shared.tile([P, 4], F32, name="bias_col", offset=65 * KB)
        w1_rows = w1.rearrange("(p j) c -> p j c", j=4)
        nc.vector.memset(w_sraw[:].bitcast(I32), 0)
        nc.vector.memset(gain_rows[:], 0.0)

        def load_w1(i):
            nc.sync.dma_start(out=w1_raw[i][:], in_=w1_rows[:, :, PASS // 2 * i : PASS // 2 * (i + 1)])

        def load_w4(b):
            rows = w4[PASS * b : PASS * (b + 1), :].rearrange("(q t e) n -> t q e n", t=4, e=4)
            for t in range(4):
                nc.sync.dma_start(out=w4_raw[b][:, t, :], in_=rows[t])

        def load_table():
            nc.sync.dma_start(out=tab_w[:].bitcast(I32), in_=tab_words[0].rearrange("p n t -> p (n t)").bitcast(I32))

        def load_w2():
            nc.sync.dma_start(out=w2_raw[:], in_=w2_words[0].bitcast(I32))

        def load_gain():
            nc.sync.dma_start(
                out=gain_rows[0:4, :].rearrange("t (g e) -> t g e", e=4),
                in_=gain.rearrange("(g t e) -> t g e", t=4, e=4),
            )

        def load_w3():
            nc.sync.dma_start(out=w3_raw[:], in_=w3_words[0].rearrange("p n t -> p (n t)").bitcast(I32))

        def load_bias():
            nc.sync.dma_start(out=bias_col[:], in_=bias.rearrange("(p s) -> p s", s=4))

        load_w1(0)
        load_w1(1)
        load_table()
        load_w1(2)
        load_scales(w_sraw, w2_scales)
        load_w1(3)
        load_scales(w_sraw, w3_scales, 4)
        load_w2()
        load_w3()
        load_gain()
        load_w4(0)
        load_w4(1)
        load_bias()

        warm_in = keep.tile([P, 1], F32, name="warm_in")
        warm_out = keep.tile([P, 1], F32, name="warm_out")
        nc.vector.memset(warm_in[:], 0.0)
        nc.scalar.activation(out=warm_out[:], in_=warm_in[:], func=ACT.Tanh)

        got_s = [None] * 3

        def gather_scales(i):
            got_s[i] = keep.tile([P, S], U8, name=f"got_s{i}", align_bytes=64)
            nc.vector.tensor_copy(got_s[i][:], tab_s[:].indirect(lists[i][:]))

        w1_q = [None, None]

        def prepare_w1(b):
            grouped = shared.tile([P, 4 * PASS], BF16, name=f"w1_grouped{b}", offset=(76 - 7 * b) * KB, align_bytes=64)
            for u in range(2):
                if b == 0:
                    dst = grouped[:].rearrange("p (t q e j) -> p q t j e", t=4, e=4, j=4)
                    src = w1_parts[2 * b + u].rearrange("p j (q t e) -> p q t j e", t=4, e=4)
                    nc.scalar.copy(out=dst[:, 16 * u : 16 * (u + 1)], in_=src)
                else:
                    dst = grouped[:].rearrange("p (t q e j) -> p q t e j", t=4, e=4, j=4)
                    src = w1_parts[2 * b + u].rearrange("p j (q t e) -> p q t e j", t=4, e=4)
                    nc.gpsimd.tensor_scalar(dst[:, 16 * u : 16 * (u + 1)], src, 1.0, 0.0, ALU.mult, ALU.add)
            codes = keep.tile([P, PASS], U32, name=f"w1_codes{b}", align_bytes=64)
            scales = keep.tile([P, PASS], U8, name=f"w1_scales{b}", align_bytes=64)
            nc.vector.quantize_mx(out=codes[:].bitcast(FP8X4), scales=scales[:], in_=grouped[:])
            w1_q[b] = (codes, scales)

        got_w = [[None] * 2 for i in range(3)]

        def gather_words(i, half, offset=None):
            if offset is None:
                g = keep.tile([P, HALF], U32, name=f"got_w{i}{half}", align_bytes=64)
            else:
                g = shared.tile([P, HALF], U32, name=f"got_w{i}{half}", offset=offset, align_bytes=64)
            nc.vector.tensor_copy(g[:], tab_w[:].indirect(lists[i][:, 32 * half : 32 * (half + 1)]))
            got_w[i][half] = g[:]

        def gather_list(i, offset):
            g = shared.tile([P, S], U32, name=f"got_w{i}", offset=offset, align_bytes=64)
            nc.vector.tensor_copy(g[:], tab_w[:].indirect(lists[i][:]))
            for half in range(2):
                got_w[i][half] = g[:, HALF * half : HALF * (half + 1)]

        def deal(name, raw, run, offset=None):
            words = raw.shape[1]
            if offset is None:
                dealt = keep.tile([P, 4 * words], U8, name=name, align_bytes=64)
            else:
                dealt = shared.tile([P, 4 * words], U8, name=name, offset=offset, align_bytes=64)
            nc.vector.tensor_copy(
                out=dealt[:].bitcast(I32).rearrange("p (b t q e) -> p b t q e", b=2, t=4, e=run),
                in_=raw.rearrange("p (b q t e) -> p b t q e", b=2, t=4, e=run),
            )
            return dealt

        gain_col = keep.tile([P, 2, 4], F32, name="gain_col")

        def spread_gain():
            gain_ps = bank("g", [P, 2, 2 * P])
            for b in range(2):
                nc.tensor.transpose(gain_ps[:, b, 0:P], gain_rows[:, P * b : P * (b + 1)], ident[:])
            nc.scalar.copy(out=gain_col[:], in_=gain_ps[:, :, 0:4])

        w4_q = [None, None]
        w4_grouped = {}

        def cast_w4(b, u, parts, eng):
            if not w4_grouped:
                both = shared.tile([P, 2 * 4 * N], BF16, name="w4_grouped", offset=22 * KB, align_bytes=64)
                w4_grouped["both"] = both[:]
                for i in range(2):
                    w4_grouped[i] = both[:, 4 * N * i : 4 * N * (i + 1)]
            dst = w4_grouped[b].rearrange("p (s m t) -> p m t s", s=4, t=4)
            src = w4_raw[b][:].rearrange("p t (m s) -> p m t s", s=4)
            share = slice(4 // parts * u, 4 // parts * (u + 1))
            if eng == "s":
                nc.scalar.copy(out=dst[:, :, :, share], in_=src[:, :, :, share])
            elif eng == "g":
                nc.gpsimd.tensor_scalar(
                    w4_grouped[b].rearrange("p (s m t) -> p m s t", s=4, t=4)[:, P // parts * u : P // parts * (u + 1)],
                    w4_raw[b][:].rearrange("p t (m s) -> p m s t", s=4)[:, P // parts * u : P // parts * (u + 1)], 1.0, 0.0, ALU.mult, ALU.add,
                )
            else:
                nc.vector.tensor_copy(out=dst[:, :, :, share], in_=src[:, :, :, share])

        def quantise_w4():
            codes = shared.tile([P, 2 * N], U32, name="w4_codes", offset=41 * KB, align_bytes=64)
            scales = shared.tile([P, 2 * N], U8, name="w4_scales", offset=40 * KB, align_bytes=64)
            nc.vector.quantize_mx(out=codes[:].bitcast(FP8X4), scales=scales[:], in_=w4_grouped["both"])
            for b in range(2):
                w4_q[b] = (codes[:, N * b : N * (b + 1)], scales[:, N * b : N * (b + 1)])

        def moving(i, j0, width):
            half, c0 = divmod(j0, HALF)
            return got_w[i][half][:, c0 : c0 + width].bitcast(FP8X4), got_s[i][:, j0 : j0 + width]

        def steps(u):
            width = UNITS[u][1]
            per_bank = HALF // width
            return [range(per_bank * n, per_bank * (n + 1)) for n in range(4 // per_bank)]

        a_sb = {}
        gated = {}
        h_grouped = {}
        h_q = {}
        dealt = {}

        def region(u):
            c0, width, b = UNITS[u]
            rhs, rhs_s = moving(0, c0, width)
            codes, scales = w1_q[b]
            for n, slices in enumerate(steps(u)):
                a_ps = bank("a", [P, HALF])
                for i, t in enumerate(slices):
                    cols = slice(P * t, P * (t + 1))
                    nc.tensor.matmul_mx(
                        out=a_ps[:, width * i : width * (i + 1)], lhsT=codes[:, cols].bitcast(FP8X4),
                        lhsT_scale=scales[:, cols], rhs=rhs, rhs_scale=rhs_s, start=True, stop=True,
                    )
                if n == 0 and u == 0:
                    a_sb[u] = shared.tile([P, 4 * width], F32, name=f"a_sb{u}", offset=40 * KB)
                elif n == 0:
                    a_sb[u] = keep.tile([P, 4 * width], F32, name=f"a_sb{u}")
                nc.scalar.copy(out=a_sb[u][:, HALF * n : HALF * (n + 1)], in_=a_ps[:])

        def gate(u):
            c0, width, b = UNITS[u]
            rhs, rhs_s = moving(1, c0, width)
            if u % 2 == 0:
                gated[u] = shared.tile([P, 4 * width], F32, name=f"gated{u}", offset=(56 - 17 * u) * KB)
            else:
                gated[u] = keep.tile([P, 4 * width], F32, name=f"gated{u}")
            for n, slices in enumerate(steps(u)):
                b_ps = bank("b", [P, HALF])
                for i, t in enumerate(slices):
                    r0 = PASS * b + P * t
                    nc.tensor.matmul_mx(
                        out=b_ps[:, width * i : width * (i + 1)], lhsT=dealt["w2_w"][:, 2 * r0 : 2 * (r0 + P)].bitcast(FP4X4),
                        lhsT_scale=dealt["w_s"][:, r0 : r0 + P], rhs=rhs, rhs_scale=rhs_s, start=True, stop=True,
                    )
                ab = a_sb[u][:, HALF * n : HALF * (n + 1)]
                nc.vector.tensor_tensor(ab, ab, b_ps[:], ALU.mult)
                if u == 0 and n == 0:
                    spread_gain()
                span = TANH_SPAN[u]
                if (n + 1) % span == 0:
                    th = a_sb[u][:, HALF * (n + 1 - span) : HALF * (n + 1)]
                    nc.scalar.activation(out=th, in_=th, func=ACT.Tanh)
                    for t in range(n + 1 - span, n + 1):
                        dst = gated[u][:, width * t : width * (t + 1)]
                        src = a_sb[u][:, width * t : width * (t + 1)]
                        g = gain_col[:, b, t : t + 1]
                        if GAIN_ENG[u][t] == "s":
                            nc.scalar.activation(out=dst, in_=src, func=ACT.Copy, scale=g)
                        else:
                            nc.gpsimd.tensor_scalar(dst, src, g, 0.0, ALU.mult, ALU.add)

        def join(c, b, first, chunks):
            u = 2 * (P * c // HALF) + b
            c0, width = UNITS[u][:2]
            if c == first and b == 0:
                h_grouped[first] = keep.tile([P, 2 * 4 * P * chunks], BF16, name=f"h_grouped{first}", align_bytes=64)
            c_ps = bank("c", [P, 4 * P])
            rhs, rhs_s = moving(2, P * c, P)
            for t in range(4):
                r0 = PASS * b + P * t
                nc.tensor.matmul_mx(
                    out=c_ps[:, P * t : P * (t + 1)], lhsT=dealt["w3_w"][:, 4 * r0 : 4 * (r0 + P)].bitcast(FP8X4),
                    lhsT_scale=dealt["w_s"][4:P, r0 : r0 + P], rhs=rhs, rhs_scale=rhs_s, start=True, stop=True,
                )
            v = b * chunks + c - first
            nc.vector.tensor_tensor(
                h_grouped[first][:, 4 * P * v : 4 * P * (v + 1)].rearrange("p (c i t) -> p c t i", i=RUN, t=4),
                gated[u][:].rearrange("p (t v c i) -> p v c t i", t=4, v=width // P, i=RUN)[:, c - c0 // P],
                c_ps[:].rearrange("p (t c i) -> p c t i", t=4, i=RUN),
                ALU.add,
            )

        def join_piece(first, chunks):
            for b in range(2):
                for c in range(first, first + chunks):
                    join(c, b, first, chunks)

        def quantise_h(first, chunks, halves):
            width = P * chunks
            count = len(halves)
            codes = keep.tile([P, width * count], U32, name=f"h_codes{first}{halves[0]}", align_bytes=64)
            scales = keep.tile([P, width * count], U8, name=f"h_scales{first}{halves[0]}", align_bytes=64)
            src = h_grouped[first][:, 4 * width * halves[0] : 4 * width * (halves[-1] + 1)]
            nc.vector.quantize_mx(out=codes[:].bitcast(FP8X4), scales=scales[:], in_=src)
            for i, b in enumerate(halves):
                h_q[b, first] = (codes, scales, width * i)

        y_scales = keep.tile([P, S], U8, name="y_scales", align_bytes=64)
        out_rows = out_0.rearrange("(p s) j -> p s j", s=4)
        out_words = out_1[0].rearrange("p m t -> p (m t)").bitcast(I32)
        y = {}

        def answer(c, chunks, evac, per_bank):
            width = P * chunks
            y[c] = keep.tile([P, 4 * width], F32, name=f"y{c}")
            for u in range(4 // per_bank):
                y_ps = bank("y" if per_bank * width == HALF else "z", [P, per_bank, width])
                for ss in range(per_bank):
                    s = per_bank * u + ss
                    for b in range(2):
                        codes, scales = w4_q[b]
                        h_codes, h_scales, h0 = h_q[b, c]
                        nc.tensor.matmul_mx(
                            out=y_ps[:, ss, :], lhsT=codes[:, P * s : P * (s + 1)].bitcast(FP8X4),
                            lhsT_scale=scales[:, P * s : P * (s + 1)], rhs=h_codes[:, h0 : h0 + width].bitcast(FP8X4),
                            rhs_scale=h_scales[:, h0 : h0 + width], start=(b == 0), stop=(b == 1),
                        )
                if evac[u] == "v":
                    s0 = per_bank * u
                    nc.vector.tensor_tensor(
                        y[c][:, width * s0 : width * (s0 + per_bank)].rearrange("p (s j) -> p s j", s=per_bank), y_ps[:],
                        bias_col[:, s0 : s0 + per_bank].unsqueeze(2).to_broadcast([P, per_bank, width]), ALU.add,
                    )
                else:
                    for ss in range(per_bank):
                        s = per_bank * u + ss
                        nc.scalar.activation(
                            out=y[c][:, width * s : width * (s + 1)], in_=y_ps[:, ss, :], func=ACT.Identity,
                            bias=bias_col[:, s : s + 1],
                        )
                if c == 4:
                    nc.sync.dma_start(
                        out=out_rows[:, 2 * u : 2 * u + 2, P * c : P * c + width],
                        in_=y[c][:, 2 * width * u : 2 * width * (u + 1)].rearrange("p (s j) -> p s j", s=2),
                    )
            if c != 4:
                nc.sync.dma_start(out=out_rows[:, :, P * c : P * c + width], in_=y[c][:].rearrange("p (s j) -> p s j", s=4))

        y_rounded = keep.tile([P, 4 * S], BF16, name="y_rounded", align_bytes=64)

        def round_y(first, c, chunks, eng):
            dst = y_rounded[:, 4 * P * c : 4 * P * (c + chunks)].rearrange("p (c i s) -> p c s i", i=4, s=4)
            src = y[first][:].rearrange("p (s c i) -> p c s i", s=4, i=4)[:, P // 4 * (c - first) : P // 4 * (c - first + chunks)]
            if eng == "s":
                nc.scalar.copy(out=dst, in_=src)
            elif eng == "g":
                nc.gpsimd.tensor_scalar(
                    y_rounded[:, 4 * P * c : 4 * P * (c + chunks)].rearrange("p (j s) -> p j s", s=4),
                    y[first][:].rearrange("p (s j) -> p j s", s=4)[:, P * (c - first) : P * (c - first + chunks)],
                    1.0, 0.0, ALU.mult, ALU.add,
                )
            else:
                nc.vector.tensor_copy(out=dst, in_=src)

        y_codes = keep.tile([P, S], U32, name="y_codes", align_bytes=64)

        def planes(c, chunks):
            cols = slice(P * c, P * (c + chunks))
            nc.vector.quantize_mx(out=y_codes[:, cols].bitcast(FP8X4), scales=y_scales[:, cols], in_=y_rounded[:, 4 * P * c : 4 * P * (c + chunks)])

        def store_words(c, chunks):
            cols = slice(P * c, P * (c + chunks))
            nc.sync.dma_start(out=out_words[:, cols], in_=y_codes[:, cols].bitcast(I32))

        gather_scales(0)
        gather_scales(1)
        gather_scales(2)
        prepare_w1(0)
        prepare_w1(1)
        gather_words(0, 0)
        gather_words(0, 1, 77 * KB)
        gather_list(1, 79 * KB)
        dealt["w_s"] = deal("w_s", w_sraw[:].bitcast(I32), 1, 37 * KB)
        dealt["w2_w"] = deal("w2_w", w2_raw[:], 2, 38 * KB)
        dealt["w3_w"] = deal("w3_w", w3_raw[:], 4, 33 * KB)
        gather_list(2, 16 * KB)
        region(0)
        region(2)
        region(1)
        region(3)
        cast_w4(0, 0, 1, "g")
        cast_w4(1, 0, 1, "g")
        for u in range(4):
            gate(u)
        quantise_w4()
        join(0, 0, 0, 2)
        join(1, 0, 0, 2)
        join(0, 1, 0, 2)
        join(1, 1, 0, 2)
        join(2, 0, 2, 2)
        quantise_h(0, 2, (0, 1))
        join(3, 0, 2, 2)
        join(2, 1, 2, 2)
        join(3, 1, 2, 2)
        join(4, 0, 4, 2)
        quantise_h(2, 2, (0, 1))
        join(5, 0, 4, 2)
        join(4, 1, 4, 2)
        join(5, 1, 4, 2)
        answer(0, 2, "ss", 2)
        round_y(0, 0, 2, "g")
        planes(0, 2)
        store_words(0, 2)
        join(6, 0, 6, 1)
        quantise_h(4, 2, (0, 1))
        join(6, 1, 6, 1)
        join(7, 0, 7, 1)
        quantise_h(6, 1, (0, 1))
        join(7, 1, 7, 1)
        quantise_h(7, 1, (0,))
        quantise_h(7, 1, (1,))
        answer(2, 2, "ss", 2)
        round_y(2, 2, 2, "s")
        answer(4, 2, "ss", 2)
        answer(6, 1, "s", 4)
        answer(7, 1, "ssss", 1)
        planes(2, 2)
        store_words(2, 2)
        round_y(4, 4, 2, "v")
        round_y(6, 6, 1, "v")
        planes(4, 2)
        store_words(4, 2)
        round_y(7, 7, 1, "v")
        planes(6, 1)
        planes(7, 1)
        store_words(6, 2)
        for q in range(4):
            queue = nc.sync if q % 2 == 0 else nc.scalar
            queue.dma_start(
                out=out_2[0, q:16:4, :].bitcast(I32), in_=y_scales[q:P:32, :].bitcast(I32)
            )
